import numpy as np
import ml_dtypes


def mxq(x, axis, fmt="e4m3"):
    dtype, down = {"e4m3": (ml_dtypes.float8_e4m3fn, 7), "e5m2": (ml_dtypes.float8_e5m2, 14)}[fmt]
    v = np.moveaxis(np.asarray(x, np.float32).astype(ml_dtypes.bfloat16).astype(np.float64), axis, -1)
    blocks = v.reshape(v.shape[:-1] + (-1, 32))
    amax = np.abs(blocks).max(-1, keepdims=True)
    byte = np.maximum(np.where(amax > 0, np.frexp(amax)[1] - 1 + 127, 0) - down, 1)
    scale = np.exp2(byte - 127.0)
    codes = (blocks / scale).astype(np.float32).astype(dtype).astype(np.float64)
    return np.moveaxis((codes * scale).reshape(v.shape), -1, axis)


WIDE = False


def mx_kscale(k):
    if not WIDE:
        return np.ones(k)
    levels = np.array([10, -10, 5, -5, 0])
    if k % 512:
        return np.exp2(np.random.permutation(np.resize(levels, k // 32))).repeat(32)
    a = np.empty((k // 512, 16))
    for p in range(k // 512):
        a[p, :8] = np.random.permutation(np.resize(levels, 8))
        for g in range(8):
            far = levels[np.abs(levels - a[p, g]) >= 10]
            a[p, g + 8] = far[np.random.randint(len(far))]
    return np.exp2(a.ravel()).repeat(32)


def f64(x):
    return np.asarray(x).astype(np.float64)


def striped(idx):
    return np.tile(idx.reshape(-1, 16).T, (8, 1)).astype(np.uint16)


def unstriped(offs):
    return offs[:16].T.reshape(-1).astype(np.int64)


E2M1 = np.array([0.0, 0.5, 1.0, 1.5, 2.0, 3.0, 4.0, 6.0, -0.0, -0.5, -1.0, -1.5, -2.0, -3.0, -4.0, -6.0])


def pack_weight(w, fmt):
    k, n = w.shape
    w = f64(np.asarray(w, np.float32).astype(ml_dtypes.bfloat16)).reshape(k // 32, 32, n)
    amax = np.abs(w).max(1)
    if fmt == "e4m3":
        byte = np.frexp(amax)[1] - 1 + 127 - 7
    else:
        mant, ex = np.frexp(amax / 6.0)
        byte = np.where(mant > 0.5, ex, ex - 1) + 127
    byte = np.clip(np.where(amax > 0, byte, 1), 1, 254)
    scaled = (w * np.exp2(127.0 - byte)[:, None, :]).reshape(k, n).astype(np.float32)
    by_word = np.ascontiguousarray(scaled.reshape(k // 512, 128, 4, n).transpose(0, 1, 3, 2))
    if fmt == "e4m3":
        words = by_word.astype(ml_dtypes.float8_e4m3fn).view(np.uint8)
    else:
        c = by_word.astype(ml_dtypes.float4_e2m1fn).view(np.uint8) & 0xF
        words = (c[..., 0::2] | (c[..., 1::2] << 4)).reshape(k // 512, 128, 2 * n)
    return np.ascontiguousarray(words), np.ascontiguousarray(byte.astype(np.uint8).reshape(k // 512, 16, n))


def unpack_weight(words, scales, fmt):
    g, _, n = scales.shape
    words = np.ascontiguousarray(words).reshape(g, 128, n, -1)
    if fmt == "e4m3":
        vals = words.view(ml_dtypes.float8_e4m3fn).astype(np.float64)
    else:
        nib = np.empty((g, 128, n, 4), np.uint8)
        nib[..., 0::2] = words & 0xF
        nib[..., 1::2] = words >> 4
        vals = E2M1[nib]
    vals = vals * np.repeat(np.exp2(scales.astype(np.float64) - 127.0), 8, axis=1)[..., None]
    return vals.transpose(0, 1, 3, 2).reshape(g * 512, n)


def gelu(v):
    return 0.5 * v * (1.0 + np.tanh(np.sqrt(2.0 / np.pi) * (v + 0.044715 * v**3)))


K, T, E, C, H, N = 512, 1024, 4, 128, 512, 512


def by_expert(wq, xq):
    return np.concatenate([wq[e].T @ xq[:, e * C:(e + 1) * C] for e in range(E)], axis=1)


def setup_inputs():
    n = np.random.standard_normal
    s = mx_kscale(K)
    u = mx_kscale(H)
    slot_token = np.random.permutation(T)[:E * C]
    x = pack_weight(n((K, T)) * s[:, None], "e4m3")
    w = [pack_weight(m, "e2m1") for m in n((E, K, N)) / np.sqrt(K) / s[None, :, None]]
    wb = [pack_weight(m, "e4m3") for m in n((E, H, N)) / np.sqrt(H) / u[None, :, None]]
    return {
        "x_words": x[0],
        "x_scales": x[1],
        "w_words": np.stack([m[0] for m in w]),
        "w_scales": np.stack([m[1] for m in w]),
        "wa": (n((E, K, H)) / np.sqrt(K) / s[None, :, None] * u).astype(np.float32),
        "wb_words": np.stack([m[0] for m in wb]),
        "wb_scales": np.stack([m[1] for m in wb]),
        "gate": np.tile(np.random.uniform(0.2, 1.0, E * C), (128, 1)).astype(np.float32),
        "offs": striped(slot_token),
    }


def reference(x_words, x_scales, w_words, w_scales, wa, wb_words, wb_scales, gate, offs):
    w = np.stack([unpack_weight(w_words[e], w_scales[e], "e2m1") for e in range(E)])
    waq = mxq(f64(wa), 1, "e4m3")
    wb = np.stack([unpack_weight(wb_words[e], wb_scales[e], "e4m3") for e in range(E)])
    idx = unstriped(offs)
    xq = unpack_weight(x_words, x_scales, "e4m3")[:, idx]
    h = gelu(by_expert(waq, xq))
    y = by_expert(w, xq) + by_expert(wb, mxq(h, 0, "e4m3"))
    out = np.zeros((N, T))
    out[:, idx] = f64(gate[:1]) * y
    return out

@@ -1,0 +1,220 @@
+from contextlib import ExitStack
+
+import concourse.mybir as mybir
+
+K, T, E, C, H, N = 512, 1024, 4, 128, 512, 512
+FLOPS = 2 * E * C * (K * H + K * N + H * N)
+
+F32 = mybir.dt.float32
+BF16 = mybir.dt.bfloat16
+I32 = mybir.dt.int32
+U32 = mybir.dt.uint32
+U16 = mybir.dt.uint16
+U8 = mybir.dt.uint8
+FP8X4 = mybir.dt.float8_e4m3fn_x4
+FP4X4 = mybir.dt.float4_e2m1fn_x4
+GELU = mybir.ActivationFunctionType.Gelu_apprx_tanh
+MULT = mybir.AluOpType.mult
+
+P = 128
+PACK = 4
+QUADS = 4
+R = N // P
+LIST_COLS = C // 16
+ALIGN = 64
+
+
+def tile_moe_elr_gelu_kernel(tc, x_words, x_scales, w_words, w_scales, wa, wb_words, wb_scales, gate, offs, out):
+    nc = tc.nc
+    with ExitStack() as ctx:
+        keep = ctx.enter_context(tc.tile_pool(name="keep", bufs=1))
+        h_psum = ctx.enter_context(tc.psum_pool(name="h_psum", bufs=2))
+        y_psum = ctx.enter_context(tc.psum_pool(name="y_psum", bufs=6))
+
+        offsets = keep.tile([P, E * LIST_COLS], U16, name="offsets")
+        x_table = keep.tile([P, T], I32, name="x_table", align_bytes=ALIGN)
+        xs_table = keep.tile([P, T], U8, name="xs_table", align_bytes=ALIGN)
+        ws_plane = keep.tile([P, E, N], U8, name="ws_plane", align_bytes=ALIGN)
+        wbs_plane = keep.tile([P, N], U8, name="wbs_plane", align_bytes=ALIGN)
+        gates = keep.tile([P, E * C], F32, name="gates", align_bytes=ALIGN)
+        windows = [keep.tile([P, T], F32, name="window%d" % r, align_bytes=ALIGN) for r in range(R)]
+        wa_raw = [keep.tile([P, PACK, H], F32, name="wa_raw%d" % e, tag="raw%d" % e, align_bytes=ALIGN) for e in range(E)]
+        w_codes = [keep.tile([P, 2 * N], U8, name="w_codes%d" % e, align_bytes=ALIGN) for e in range(E)]
+        wb_codes = [keep.tile([P, N], I32, name="wb_codes%d" % e, align_bytes=ALIGN) for e in range(E)]
+        warm = keep.tile([P, 2], F32, name="warm", align_bytes=ALIGN)
+
+        nc.vector.memset(warm[:, 0:1], 0.0)
+        nc.vector.memset(ws_plane[:].rearrange("p e n -> p (e n)").bitcast(I32), 0)
+        nc.vector.memset(wbs_plane[:].bitcast(I32), 0)
+        nc.scalar.activation(warm[:, 1:2], warm[:, 0:1], GELU)
+        for r in range(R):
+            nc.vector.memset(windows[r][:], 0.0)
+
+        def load_wa(e):
+            nc.sync.dma_start(out=wa_raw[e][:], in_=wa[e].rearrange("(p j) c -> p j c", j=PACK))
+
+        def load_w(e):
+            nc.sync.dma_start(out=w_codes[e][:].bitcast(I32), in_=w_words[e, 0].bitcast(I32))
+
+        def load_wb(e):
+            nc.sync.dma_start(out=wb_codes[e][:], in_=wb_words[e, 0].rearrange("p n d -> p (n d)").bitcast(I32))
+
+        def load_xs(q):
+            rows = x_scales[0, 4 * q : 4 * q + 4, :].bitcast(I32)
+            nc.sync.dma_start(out=xs_table[32 * q : 32 * q + 32, :].bitcast(I32), in_=rows.partition_broadcast(8))
+
+        def load_ws(q):
+            rows = w_scales[:, 0, 4 * q : 4 * q + 4, :].bitcast(I32).rearrange("e b n -> b e n")
+            nc.sync.dma_start(out=ws_plane[32 * q : 32 * q + 4, :, :].bitcast(I32), in_=rows)
+
+        def load_wbs(q):
+            rows = wb_scales[:, 0, 4 * q : 4 * q + 4, :].bitcast(I32)
+            nc.sync.dma_start(out=wbs_plane[32 * q : 32 * q + 16, :].bitcast(I32), in_=rows)
+
+        load_wa(0)
+        for q in range(3):
+            load_xs(q)
+        nc.sync.dma_start(out=x_table[:], in_=x_words[0].rearrange("p t d -> p (t d)").bitcast(I32))
+        load_xs(3)
+        nc.sync.dma_start(offsets[:], offs)
+        load_ws(0)
+        load_wb(0)
+        for q in range(1, QUADS):
+            load_ws(q)
+        load_w(0)
+        for q in range(QUADS):
+            load_wbs(q)
+        load_wa(1)
+        nc.sync.dma_start(out=gates[:], in_=gate)
+        for e in range(2, E):
+            load_wa(e)
+            load_w(e - 1)
+            load_wb(e - 1)
+        load_w(E - 1)
+        load_wb(E - 1)
+
+        slot_words = {}
+        slot_scales = {}
+        wa_codes = {}
+        wa_scales = {}
+        h_codes = {}
+        h_scales = {}
+
+        def gather(first, last):
+            n = (last - first) * C
+            cols = offsets[:, first * LIST_COLS : last * LIST_COLS]
+            words = keep.tile([P, n], U32, name="slot_words%d" % first, align_bytes=ALIGN)
+            scales = keep.tile([P, n], U8, name="slot_scales%d" % first, align_bytes=ALIGN)
+            nc.vector.tensor_copy(words[:], x_table[:].bitcast(U32).indirect(cols))
+            nc.vector.tensor_copy(scales[:], xs_table[:].indirect(cols))
+            for e in range(first, last):
+                own = slice((e - first) * C, (e - first + 1) * C)
+                slot_words[e] = words[:, own].bitcast(FP8X4)
+                slot_scales[e] = scales[:, own]
+
+        def cast_half(e, half, copy):
+            grouped = keep.tile([P, 2, P, PACK], BF16, name="grouped%d_%d" % (e, half), align_bytes=ALIGN)
+            source = wa_raw[e][:].rearrange("p j (m t) -> p m j t", t=PACK)[:, :, :, 2 * half : 2 * half + 2]
+            copy(grouped[:].rearrange("p t m j -> p m j t"), source)
+            return grouped
+
+        def quantize_half(e, half, grouped):
+            codes = keep.tile([P, 2 * P], U32, name="wa_codes%d_%d" % (e, half), tag="wac%d_%d" % (e, half), align_bytes=ALIGN)
+            scales = keep.tile([P, 2 * P], U8, name="wa_scales%d_%d" % (e, half), align_bytes=ALIGN)
+            nc.vector.quantize_mx(out=codes[:].bitcast(FP8X4), scales=scales[:], in_=grouped[:].rearrange("p t m j -> p (t m j)"))
+            wa_codes[e, half] = codes
+            wa_scales[e, half] = scales
+
+        def prepare(e):
+            first = cast_half(e, 0, nc.vector.tensor_copy if e < 2 else nc.scalar.copy)
+            second = cast_half(e, 1, nc.scalar.copy)
+            quantize_half(e, 0, first)
+            if e == 0:
+                gather(0, 1)
+            quantize_half(e, 1, second)
+
+        def hidden(e):
+            bank = h_psum.tile([P, PACK, C], F32, name="h_bank")
+            for t in range(PACK):
+                cols = slice((t % 2) * P, (t % 2 + 1) * P)
+                nc.tensor.matmul_mx(
+                    out=bank[:, t, :],
+                    lhsT=wa_codes[e, t // 2][:, cols].bitcast(FP8X4),
+                    lhsT_scale=wa_scales[e, t // 2][:, cols],
+                    rhs=slot_words[e],
+                    rhs_scale=slot_scales[e],
+                    start=True,
+                    stop=True,
+                )
+            rounded = keep.tile([P, C, PACK], BF16, name="h_rounded%d" % e, align_bytes=ALIGN)
+            nc.scalar.activation(rounded[:], bank[:].rearrange("p t n -> p n t"), GELU)
+            codes = keep.tile([P, C], U32, name="h_codes%d" % e, align_bytes=ALIGN)
+            scales = keep.tile([P, C], U8, name="h_scales%d" % e, align_bytes=ALIGN)
+            nc.vector.quantize_mx(out=codes[:].bitcast(FP8X4), scales=scales[:], in_=rounded[:].rearrange("p n t -> p (n t)"))
+            h_codes[e] = codes
+            h_scales[e] = scales
+
+        def product(e, r):
+            bank = y_psum.tile([P, 4 * C], F32, name="y_bank")
+            cols = slice(r * P, (r + 1) * P)
+            nc.tensor.matmul_mx(
+                out=bank[:, 0:C],
+                lhsT=w_codes[e][:, 2 * r * P : 2 * (r + 1) * P].bitcast(FP4X4),
+                lhsT_scale=ws_plane[:, e, cols],
+                rhs=slot_words[e],
+                rhs_scale=slot_scales[e],
+                start=True,
+                stop=False,
+            )
+            nc.tensor.matmul_mx(
+                out=bank[:, 0:C],
+                lhsT=wb_codes[e][:, cols].bitcast(FP8X4),
+                lhsT_scale=wbs_plane[4 * e : P, cols],
+                rhs=h_codes[e][:].bitcast(FP8X4),
+                rhs_scale=h_scales[e][:],
+                start=False,
+                stop=True,
+            )
+            return bank
+
+        def scatter(r, first, last, values):
+            cols = offsets[:, first * LIST_COLS : last * LIST_COLS]
+            nc.vector.tensor_tensor(windows[r][:].indirect(cols), values, gates[:, first * C : last * C], MULT)
+
+        def send(e, rows, banks, tag):
+            staged = keep.tile([P, len(rows), C], F32, name="staged%d_%d" % (e, rows[0]), tag=tag, align_bytes=ALIGN)
+            for i, r in enumerate(rows):
+                nc.scalar.copy(staged[:, i, :], banks[r][:, 0:C])
+                scatter(r, e, e + 1, staged[:, i, :])
+
+        def store(r):
+            nc.sync.dma_start(out=out[r * P : (r + 1) * P, :], in_=windows[r][:])
+
+        prepare(0)
+        hidden(0)
+        gather(1, E)
+        banks = [product(0, r) for r in range(R)]
+        send(0, [0], banks, "own0")
+        prepare(1)
+        send(0, [1, 2], banks, "raw1")
+        hidden(1)
+        send(0, [3], banks, "wac1_1")
+        banks = [product(1, r) for r in range(R)]
+        prepare(2)
+        send(1, [0, 1, 2], banks, "raw2")
+        hidden(2)
+        send(1, [3], banks, "wac2_1")
+        banks = [product(2, r) for r in range(R)]
+        prepare(3)
+        send(2, [0, 1], banks, "raw3")
+        hidden(3)
+        send(2, [2], banks, "wac3_1")
+        last_rows = keep.tile([P, 2 * C], F32, name="last_rows", align_bytes=ALIGN)
+        nc.scalar.copy(last_rows[:, 0:C], banks[3][:, 0:C])
+        banks = [product(3, r) for r in range(R)]
+        for r in range(R - 1):
+            send(3, [r], banks, "own3_%d" % r)
+            store(r)
+        nc.scalar.copy(last_rows[:, C : 2 * C], banks[3][:, 0:C])
+        scatter(3, 2, 4, last_rows[:])
+        store(3)

@@ -22,36 +22,46 @@ QUADS = 4
 R = N // P
 LIST_COLS = C // 16
 ALIGN = 64
+H_BANK = (0, 1, 2, 5)
+Y_BANK = ((1, 2, 3, 4), (0, 5, 6, 7), (3, 1, 4, 0), (2, 6, 7, 3))
 
 
 def tile_moe_elr_gelu_kernel(tc, x_words, x_scales, w_words, w_scales, wa, wb_words, wb_scales, gate, offs, out):
     nc = tc.nc
     with ExitStack() as ctx:
         keep = ctx.enter_context(tc.tile_pool(name="keep", bufs=1))
-        h_psum = ctx.enter_context(tc.psum_pool(name="h_psum", bufs=2))
-        y_psum = ctx.enter_context(tc.psum_pool(name="y_psum", bufs=6))
+        psum = ctx.enter_context(tc.psum_pool(name="psum", bufs=1))
 
         offsets = keep.tile([P, E * LIST_COLS], U16, name="offsets")
         x_table = keep.tile([P, T], I32, name="x_table", align_bytes=ALIGN)
         xs_table = keep.tile([P, T], U8, name="xs_table", align_bytes=ALIGN)
         ws_plane = keep.tile([P, E, N], U8, name="ws_plane", align_bytes=ALIGN)
         wbs_plane = keep.tile([P, N], U8, name="wbs_plane", align_bytes=ALIGN)
-        gates = keep.tile([P, E * C], F32, name="gates", align_bytes=ALIGN)
+        first_gates = keep.tile([P, C], F32, name="first_gates", align_bytes=ALIGN)
+        later_gates = keep.tile([P, (E - 1) * C], F32, name="later_gates", align_bytes=ALIGN)
         windows = [keep.tile([P, T], F32, name="window%d" % r, align_bytes=ALIGN) for r in range(R)]
-        wa_raw = [keep.tile([P, PACK, H], F32, name="wa_raw%d" % e, tag="raw%d" % e, align_bytes=ALIGN) for e in range(E)]
+        wa_raw = [keep.tile([P, PACK, H], F32, name="wa_raw%d" % e, tag="raw%d" % e, align_bytes=ALIGN) for e in range(1)]
+        wa_cols = {
+            (e, side): keep.tile([P, PACK, H // 2], F32, name="wa_cols%d_%d" % (e, side), tag="raw%d_%d" % (e, side), align_bytes=ALIGN)
+            for e in range(1, E)
+            for side in range(2)
+        }
         w_codes = [keep.tile([P, 2 * N], U8, name="w_codes%d" % e, align_bytes=ALIGN) for e in range(E)]
         wb_codes = [keep.tile([P, N], I32, name="wb_codes%d" % e, align_bytes=ALIGN) for e in range(E)]
-        warm = keep.tile([P, 2], F32, name="warm", align_bytes=ALIGN)
 
-        nc.vector.memset(warm[:, 0:1], 0.0)
         nc.vector.memset(ws_plane[:].rearrange("p e n -> p (e n)").bitcast(I32), 0)
-        nc.vector.memset(wbs_plane[:].bitcast(I32), 0)
-        nc.scalar.activation(warm[:, 1:2], warm[:, 0:1], GELU)
-        for r in range(R):
+        nc.gpsimd.memset(xs_table[:].bitcast(I32), 0)
+        nc.gpsimd.memset(wbs_plane[:].bitcast(I32), 0)
+        for r in range(2):
             nc.vector.memset(windows[r][:], 0.0)
+            nc.scalar.activation(windows[r + 2][:], windows[r][:], GELU)
 
         def load_wa(e):
             nc.sync.dma_start(out=wa_raw[e][:], in_=wa[e].rearrange("(p j) c -> p j c", j=PACK))
+
+        def load_wa_side(e, side):
+            cols = slice(side * H // 2, (side + 1) * H // 2)
+            nc.sync.dma_start(out=wa_cols[e, side][:], in_=wa[e].rearrange("(p j) c -> p j c", j=PACK)[:, :, cols])
 
         def load_w(e):
             nc.sync.dma_start(out=w_codes[e][:].bitcast(I32), in_=w_words[e, 0].bitcast(I32))
@@ -61,7 +71,7 @@ def tile_moe_elr_gelu_kernel(tc, x_words, x_scales, w_words, w_scales, wa, wb_wo
 
         def load_xs(q):
             rows = x_scales[0, 4 * q : 4 * q + 4, :].bitcast(I32)
-            nc.sync.dma_start(out=xs_table[32 * q : 32 * q + 32, :].bitcast(I32), in_=rows.partition_broadcast(8))
+            nc.sync.dma_start(out=xs_table[32 * q : 32 * q + 4, :].bitcast(I32), in_=rows)
 
         def load_ws(q):
             rows = w_scales[:, 0, 4 * q : 4 * q + 4, :].bitcast(I32).rearrange("e b n -> b e n")
@@ -69,27 +79,29 @@ def tile_moe_elr_gelu_kernel(tc, x_words, x_scales, w_words, w_scales, wa, wb_wo
 
         def load_wbs(q):
             rows = wb_scales[:, 0, 4 * q : 4 * q + 4, :].bitcast(I32)
-            nc.sync.dma_start(out=wbs_plane[32 * q : 32 * q + 16, :].bitcast(I32), in_=rows)
+            nc.gpsimd.dma_start(out=wbs_plane[32 * q : 32 * q + 16, :].bitcast(I32), in_=rows)
 
-        load_wa(0)
-        for q in range(3):
-            load_xs(q)
-        nc.sync.dma_start(out=x_table[:], in_=x_words[0].rearrange("p t d -> p (t d)").bitcast(I32))
-        load_xs(3)
-        nc.sync.dma_start(offsets[:], offs)
-        load_ws(0)
-        load_wb(0)
-        for q in range(1, QUADS):
-            load_ws(q)
-        load_w(0)
         for q in range(QUADS):
             load_wbs(q)
-        load_wa(1)
-        nc.sync.dma_start(out=gates[:], in_=gate)
+        nc.sync.dma_start(out=x_table[:], in_=x_words[0].rearrange("p t d -> p (t d)").bitcast(I32))
+        nc.sync.dma_start(offsets[:], offs)
+        for q in range(QUADS):
+            load_xs(q)
+        load_wa(0)
+        load_wa_side(1, 0)
+        for q in range(QUADS):
+            load_ws(q)
+        load_wa_side(1, 1)
+        load_w(0)
+        load_wb(0)
+        nc.sync.dma_start(out=first_gates[:], in_=gate[:, 0:C])
         for e in range(2, E):
-            load_wa(e)
+            load_wa_side(e, 0)
             load_w(e - 1)
             load_wb(e - 1)
+            load_wa_side(e, 1)
+            if e == 2:
+                nc.sync.dma_start(out=later_gates[:], in_=gate[:, C : E * C])
         load_w(E - 1)
         load_wb(E - 1)
 
@@ -99,42 +111,49 @@ def tile_moe_elr_gelu_kernel(tc, x_words, x_scales, w_words, w_scales, wa, wb_wo
         wa_scales = {}
         h_codes = {}
         h_scales = {}
+        banks = {}
 
-        def gather(first, last):
-            n = (last - first) * C
-            cols = offsets[:, first * LIST_COLS : last * LIST_COLS]
-            words = keep.tile([P, n], U32, name="slot_words%d" % first, align_bytes=ALIGN)
-            scales = keep.tile([P, n], U8, name="slot_scales%d" % first, align_bytes=ALIGN)
-            nc.vector.tensor_copy(words[:], x_table[:].bitcast(U32).indirect(cols))
-            nc.vector.tensor_copy(scales[:], xs_table[:].indirect(cols))
-            for e in range(first, last):
-                own = slice((e - first) * C, (e - first + 1) * C)
+        def gather():
+            words = keep.tile([P, E * C], U32, name="slot_words", align_bytes=ALIGN)
+            scales = keep.tile([P, E * C], U8, name="slot_scales", align_bytes=ALIGN)
+            nc.vector.tensor_copy(words[:], x_table[:].bitcast(U32).indirect(offsets[:]))
+            nc.vector.tensor_copy(scales[:], xs_table[:].indirect(offsets[:]))
+            for e in range(E):
+                own = slice(e * C, (e + 1) * C)
                 slot_words[e] = words[:, own].bitcast(FP8X4)
                 slot_scales[e] = scales[:, own]
 
         def cast_half(e, half, copy):
-            grouped = keep.tile([P, 2, P, PACK], BF16, name="grouped%d_%d" % (e, half), align_bytes=ALIGN)
+            grouped = keep.tile([P, 2, P, PACK], BF16, name="grouped%d_%d" % (e, half), tag="grouped%d_%d" % (e, half), align_bytes=ALIGN)
             source = wa_raw[e][:].rearrange("p j (m t) -> p m j t", t=PACK)[:, :, :, 2 * half : 2 * half + 2]
             copy(grouped[:].rearrange("p t m j -> p m j t"), source)
-            return grouped
+            return grouped[:]
 
         def quantize_half(e, half, grouped):
             codes = keep.tile([P, 2 * P], U32, name="wa_codes%d_%d" % (e, half), tag="wac%d_%d" % (e, half), align_bytes=ALIGN)
             scales = keep.tile([P, 2 * P], U8, name="wa_scales%d_%d" % (e, half), align_bytes=ALIGN)
-            nc.vector.quantize_mx(out=codes[:].bitcast(FP8X4), scales=scales[:], in_=grouped[:].rearrange("p t m j -> p (t m j)"))
+            nc.vector.quantize_mx(out=codes[:].bitcast(FP8X4), scales=scales[:], in_=grouped.rearrange("p t m j -> p (t m j)"))
             wa_codes[e, half] = codes
             wa_scales[e, half] = scales
 
         def prepare(e):
-            first = cast_half(e, 0, nc.vector.tensor_copy if e < 2 else nc.scalar.copy)
+            first = cast_half(e, 0, nc.vector.tensor_copy)
             second = cast_half(e, 1, nc.scalar.copy)
             quantize_half(e, 0, first)
-            if e == 0:
-                gather(0, 1)
             quantize_half(e, 1, second)
 
-        def hidden(e):
-            bank = h_psum.tile([P, PACK, C], F32, name="h_bank")
+        def cast_side(e, side, grouped, copy):
+            half_m = P // 2
+            source = wa_cols[e, side][:].rearrange("p j (m u t) -> p u m j t", u=2, t=2)
+            target = grouped[:, :, side * half_m : (side + 1) * half_m, :].rearrange("p (u t) m j -> p u m j t", u=2)
+            copy(target, source)
+
+        def quantize_both(e, grouped):
+            for half in range(2):
+                quantize_half(e, half, grouped[:, 2 * half : 2 * half + 2, :, :])
+
+        def hidden(e, rounded, codes_tag):
+            bank = psum.tile([P, PACK, C], F32, name="h_bank%d" % e, tag="bank%d" % H_BANK[e])
             for t in range(PACK):
                 cols = slice((t % 2) * P, (t % 2 + 1) * P)
                 nc.tensor.matmul_mx(
@@ -146,16 +165,15 @@ def tile_moe_elr_gelu_kernel(tc, x_words, x_scales, w_words, w_scales, wa, wb_wo
                     start=True,
                     stop=True,
                 )
-            rounded = keep.tile([P, C, PACK], BF16, name="h_rounded%d" % e, align_bytes=ALIGN)
-            nc.scalar.activation(rounded[:], bank[:].rearrange("p t n -> p n t"), GELU)
-            codes = keep.tile([P, C], U32, name="h_codes%d" % e, align_bytes=ALIGN)
+            nc.scalar.activation(rounded.rearrange("p (n t) -> p n t", t=PACK), bank[:].rearrange("p t n -> p n t"), GELU)
+            codes = keep.tile([P, C], U32, name="h_codes%d" % e, tag=codes_tag, align_bytes=ALIGN)
             scales = keep.tile([P, C], U8, name="h_scales%d" % e, align_bytes=ALIGN)
-            nc.vector.quantize_mx(out=codes[:].bitcast(FP8X4), scales=scales[:], in_=rounded[:].rearrange("p n t -> p (n t)"))
+            nc.vector.quantize_mx(out=codes[:].bitcast(FP8X4), scales=scales[:], in_=rounded)
             h_codes[e] = codes
             h_scales[e] = scales
 
         def product(e, r):
-            bank = y_psum.tile([P, 4 * C], F32, name="y_bank")
+            bank = psum.tile([P, 4 * C], F32, name="y_bank%d_%d" % (e, r), tag="bank%d" % Y_BANK[e][r])
             cols = slice(r * P, (r + 1) * P)
             nc.tensor.matmul_mx(
                 out=bank[:, 0:C],
@@ -179,42 +197,53 @@ def tile_moe_elr_gelu_kernel(tc, x_words, x_scales, w_words, w_scales, wa, wb_wo
 
         def scatter(r, first, last, values):
             cols = offsets[:, first * LIST_COLS : last * LIST_COLS]
-            nc.vector.tensor_tensor(windows[r][:].indirect(cols), values, gates[:, first * C : last * C], MULT)
+            weights = first_gates[:] if first == 0 else later_gates[:, (first - 1) * C : (last - 1) * C]
+            nc.vector.tensor_tensor(windows[r][:].indirect(cols), values, weights, MULT)
 
-        def send(e, rows, banks, tag):
-            staged = keep.tile([P, len(rows), C], F32, name="staged%d_%d" % (e, rows[0]), tag=tag, align_bytes=ALIGN)
-            for i, r in enumerate(rows):
-                nc.scalar.copy(staged[:, i, :], banks[r][:, 0:C])
-                scatter(r, e, e + 1, staged[:, i, :])
+        def room(name, tag, blocks):
+            return keep.tile([P, blocks * C], F32, name=name, tag=tag, align_bytes=ALIGN)
+
+        def send(blocks, staged):
+            for i, (e, r) in enumerate(blocks):
+                cols = slice(i * C, (i + 1) * C)
+                nc.scalar.copy(staged[:, cols], banks[e, r][:, 0:C])
+                scatter(r, e, e + 1, staged[:, cols])
+
+        def products(e):
+            for r in range(R):
+                banks[e, r] = product(e, r)
 
         def store(r):
             nc.sync.dma_start(out=out[r * P : (r + 1) * P, :], in_=windows[r][:])
 
+        grouped = {e: keep.tile([P, PACK, P, PACK], BF16, name="grouped%d" % e, tag="grouped%d" % e, align_bytes=ALIGN) for e in range(1, E)}
+        gather()
         prepare(0)
-        hidden(0)
-        gather(1, E)
-        banks = [product(0, r) for r in range(R)]
-        send(0, [0], banks, "own0")
-        prepare(1)
-        send(0, [1, 2], banks, "raw1")
-        hidden(1)
-        send(0, [3], banks, "wac1_1")
-        banks = [product(1, r) for r in range(R)]
-        prepare(2)
-        send(1, [0, 1, 2], banks, "raw2")
-        hidden(2)
-        send(1, [3], banks, "wac2_1")
-        banks = [product(2, r) for r in range(R)]
-        prepare(3)
-        send(2, [0, 1], banks, "raw3")
-        hidden(3)
-        send(2, [2], banks, "wac3_1")
-        last_rows = keep.tile([P, 2 * C], F32, name="last_rows", align_bytes=ALIGN)
-        nc.scalar.copy(last_rows[:, 0:C], banks[3][:, 0:C])
-        banks = [product(3, r) for r in range(R)]
+        for side in range(2):
+            cast_side(1, side, grouped[1], nc.vector.tensor_copy)
+        hidden(0, room("h0", "h0", 2)[:].bitcast(BF16), "raw1_1")
+        quantize_both(1, grouped[1])
+        products(0)
+        send([(0, 0), (0, 1), (0, 2)], room("early0", "early0", 3))
+        with_gelu = {1: [(0, 3)], 2: [(1, 2)]}
+        after_cast = {1: [(1, 0), (1, 1)], 2: [(1, 3), (2, 0)]}
+        for e in range(1, E - 1):
+            cast_side(e + 1, 0, grouped[e + 1], nc.scalar.copy)
+            shared = room("shared%d" % e, "raw%d_0" % (e + 1), 3)
+            hidden(e, shared[:, 0 : 2 * C].bitcast(BF16), "hc%d" % e)
+            send(with_gelu[e], shared[:, 2 * C :])
+            products(e)
+            cast_side(e + 1, 1, grouped[e + 1], nc.scalar.copy)
+            quantize_both(e + 1, grouped[e + 1])
+            send(after_cast[e], room("after%d" % e, "raw%d_1" % (e + 1), 2))
+        hidden(3, room("h3", "h3", 2)[:].bitcast(BF16), "hc3")
+        send([(2, 1), (2, 2)], room("late2", "wac3_1", 2))
+        last_rows = room("last_rows", "wac3_0", 2)
+        nc.scalar.copy(last_rows[:, 0:C], banks[2, 3][:, 0:C])
+        products(3)
         for r in range(R - 1):
-            send(3, [r], banks, "own3_%d" % r)
+            send([(3, r)], room("own3_%d" % r, "own3_%d" % r, 1))
             store(r)
-        nc.scalar.copy(last_rows[:, C : 2 * C], banks[3][:, 0:C])
+        nc.scalar.copy(last_rows[:, C : 2 * C], banks[3, 3][:, 0:C])
         scatter(3, 2, 4, last_rows[:])
         store(3)

@@ -22,8 +22,7 @@ QUADS = 4
 R = N // P
 LIST_COLS = C // 16
 ALIGN = 64
-H_BANK = (0, 1, 2, 5)
-Y_BANK = ((1, 2, 3, 4), (0, 5, 6, 7), (3, 1, 4, 0), (2, 6, 7, 3))
+HALF_M = P // 2
 
 
 def tile_moe_elr_gelu_kernel(tc, x_words, x_scales, w_words, w_scales, wa, wb_words, wb_scales, gate, offs, out):
@@ -32,36 +31,31 @@ def tile_moe_elr_gelu_kernel(tc, x_words, x_scales, w_words, w_scales, wa, wb_wo
         keep = ctx.enter_context(tc.tile_pool(name="keep", bufs=1))
         psum = ctx.enter_context(tc.psum_pool(name="psum", bufs=1))
 
-        offsets = keep.tile([P, E * LIST_COLS], U16, name="offsets")
-        x_table = keep.tile([P, T], I32, name="x_table", align_bytes=ALIGN)
-        xs_table = keep.tile([P, T], U8, name="xs_table", align_bytes=ALIGN)
-        ws_plane = keep.tile([P, E, N], U8, name="ws_plane", align_bytes=ALIGN)
-        wbs_plane = keep.tile([P, N], U8, name="wbs_plane", align_bytes=ALIGN)
-        first_gates = keep.tile([P, C], F32, name="first_gates", align_bytes=ALIGN)
-        later_gates = keep.tile([P, (E - 1) * C], F32, name="later_gates", align_bytes=ALIGN)
-        windows = [keep.tile([P, T], F32, name="window%d" % r, align_bytes=ALIGN) for r in range(R)]
-        wa_raw = [keep.tile([P, PACK, H], F32, name="wa_raw%d" % e, tag="raw%d" % e, align_bytes=ALIGN) for e in range(1)]
-        wa_cols = {
-            (e, side): keep.tile([P, PACK, H // 2], F32, name="wa_cols%d_%d" % (e, side), tag="raw%d_%d" % (e, side), align_bytes=ALIGN)
-            for e in range(1, E)
-            for side in range(2)
-        }
-        w_codes = [keep.tile([P, 2 * N], U8, name="w_codes%d" % e, align_bytes=ALIGN) for e in range(E)]
-        wb_codes = [keep.tile([P, N], I32, name="wb_codes%d" % e, align_bytes=ALIGN) for e in range(E)]
+        def sb(shape, dtype, name, tag=None):
+            return keep.tile(shape, dtype, name=name, tag=tag or name, align_bytes=ALIGN)
 
+        offsets = keep.tile([P, E * LIST_COLS], U16, name="offsets")
+        x_table = sb([P, T], I32, "x_table")
+        xs_table = sb([P, T], U8, "xs_table")
+        ws_plane = sb([P, E, N], U8, "ws_plane")
+        wbs_plane = sb([P, N], U8, "wbs_plane")
+        first_gates = sb([P, C], F32, "first_gates")
+        later_gates = sb([P, (E - 1) * C], F32, "later_gates")
+        windows = [sb([P, T], F32, "window%d" % r) for r in range(R)]
+        wa_raw = [sb([P, PACK, H], F32, "raw%d" % e) for e in range(E)]
+        w_codes = [sb([P, 2 * N], U8, "w_codes%d" % e) for e in range(E)]
+        wb_codes = [sb([P, N], I32, "wb_codes%d" % e) for e in range(E)]
+
+        nc.vector.memset(xs_table[:].bitcast(I32), 0)
+        nc.vector.memset(windows[0][:], 0.0)
         nc.vector.memset(ws_plane[:].rearrange("p e n -> p (e n)").bitcast(I32), 0)
-        nc.gpsimd.memset(xs_table[:].bitcast(I32), 0)
-        nc.gpsimd.memset(wbs_plane[:].bitcast(I32), 0)
-        for r in range(2):
-            nc.vector.memset(windows[r][:], 0.0)
-            nc.scalar.activation(windows[r + 2][:], windows[r][:], GELU)
+        nc.vector.memset(wbs_plane[:].bitcast(I32), 0)
+        nc.vector.tensor_copy(windows[1][:], windows[0][:])
+        for r in (2, 3):
+            nc.scalar.activation(windows[r][:], windows[0][:], GELU)
 
         def load_wa(e):
             nc.sync.dma_start(out=wa_raw[e][:], in_=wa[e].rearrange("(p j) c -> p j c", j=PACK))
-
-        def load_wa_side(e, side):
-            cols = slice(side * H // 2, (side + 1) * H // 2)
-            nc.sync.dma_start(out=wa_cols[e, side][:], in_=wa[e].rearrange("(p j) c -> p j c", j=PACK)[:, :, cols])
 
         def load_w(e):
             nc.sync.dma_start(out=w_codes[e][:].bitcast(I32), in_=w_words[e, 0].bitcast(I32))
@@ -79,171 +73,165 @@ def tile_moe_elr_gelu_kernel(tc, x_words, x_scales, w_words, w_scales, wa, wb_wo
 
         def load_wbs(q):
             rows = wb_scales[:, 0, 4 * q : 4 * q + 4, :].bitcast(I32)
-            nc.gpsimd.dma_start(out=wbs_plane[32 * q : 32 * q + 16, :].bitcast(I32), in_=rows)
+            nc.sync.dma_start(out=wbs_plane[32 * q : 32 * q + 16, :].bitcast(I32), in_=rows)
 
-        for q in range(QUADS):
-            load_wbs(q)
         nc.sync.dma_start(out=x_table[:], in_=x_words[0].rearrange("p t d -> p (t d)").bitcast(I32))
         nc.sync.dma_start(offsets[:], offs)
         for q in range(QUADS):
             load_xs(q)
         load_wa(0)
-        load_wa_side(1, 0)
+        nc.sync.dma_start(out=first_gates[:], in_=gate[:, 0:C])
         for q in range(QUADS):
             load_ws(q)
-        load_wa_side(1, 1)
+        load_wa(1)
         load_w(0)
         load_wb(0)
-        nc.sync.dma_start(out=first_gates[:], in_=gate[:, 0:C])
-        for e in range(2, E):
-            load_wa_side(e, 0)
-            load_w(e - 1)
-            load_wb(e - 1)
-            load_wa_side(e, 1)
-            if e == 2:
-                nc.sync.dma_start(out=later_gates[:], in_=gate[:, C : E * C])
-        load_w(E - 1)
-        load_wb(E - 1)
+        for q in range(QUADS):
+            load_wbs(q)
+        load_wa(2)
+        load_w(1)
+        load_wb(1)
+        nc.sync.dma_start(out=later_gates[:], in_=gate[:, C : E * C])
+        load_wa(3)
+        for e in (2, 3):
+            load_w(e)
+            load_wb(e)
 
-        slot_words = {}
-        slot_scales = {}
-        wa_codes = {}
-        wa_scales = {}
+        words = sb([P, E * C], U32, "slot_words")
+        word_scales = sb([P, E * C], U8, "slot_scales")
+        nc.vector.tensor_copy(words[:], x_table[:].bitcast(U32).indirect(offsets[:]))
+        nc.vector.tensor_copy(word_scales[:], xs_table[:].indirect(offsets[:]))
+
+        wa_codes = [sb([P, H], U32, "wac%d" % e) for e in range(E)]
+        wa_scales = [sb([P, H], U8, "was%d" % e) for e in range(E)]
         h_codes = {}
         h_scales = {}
         banks = {}
 
-        def gather():
-            words = keep.tile([P, E * C], U32, name="slot_words", align_bytes=ALIGN)
-            scales = keep.tile([P, E * C], U8, name="slot_scales", align_bytes=ALIGN)
-            nc.vector.tensor_copy(words[:], x_table[:].bitcast(U32).indirect(offsets[:]))
-            nc.vector.tensor_copy(scales[:], xs_table[:].indirect(offsets[:]))
-            for e in range(E):
-                own = slice(e * C, (e + 1) * C)
-                slot_words[e] = words[:, own].bitcast(FP8X4)
-                slot_scales[e] = scales[:, own]
+        def quantize(e, first, count, values):
+            cols = slice(first, first + count)
+            nc.vector.quantize_mx(out=wa_codes[e][:, cols].bitcast(FP8X4), scales=wa_scales[e][:, cols], in_=values)
 
-        def cast_half(e, half, copy):
-            grouped = keep.tile([P, 2, P, PACK], BF16, name="grouped%d_%d" % (e, half), tag="grouped%d_%d" % (e, half), align_bytes=ALIGN)
-            source = wa_raw[e][:].rearrange("p j (m t) -> p m j t", t=PACK)[:, :, :, 2 * half : 2 * half + 2]
-            copy(grouped[:].rearrange("p t m j -> p m j t"), source)
-            return grouped[:]
+        def cast_pair(e, u, copy, tag=None):
+            pair = sb([P, 2, P, PACK], BF16, "grouped%d_%d" % (e, u), tag)
+            source = wa_raw[e][:].rearrange("p j (m t) -> p m j t", t=PACK)[:, :, :, 2 * u : 2 * u + 2]
+            copy(pair[:].rearrange("p t m j -> p m j t"), source)
+            return pair
 
-        def quantize_half(e, half, grouped):
-            codes = keep.tile([P, 2 * P], U32, name="wa_codes%d_%d" % (e, half), tag="wac%d_%d" % (e, half), align_bytes=ALIGN)
-            scales = keep.tile([P, 2 * P], U8, name="wa_scales%d_%d" % (e, half), align_bytes=ALIGN)
-            nc.vector.quantize_mx(out=codes[:].bitcast(FP8X4), scales=scales[:], in_=grouped.rearrange("p t m j -> p (t m j)"))
-            wa_codes[e, half] = codes
-            wa_scales[e, half] = scales
+        def quantize_pair(e, u, pair):
+            quantize(e, 2 * u * P, 2 * P, pair[:].rearrange("p t m j -> p (t m j)"))
 
-        def prepare(e):
-            first = cast_half(e, 0, nc.vector.tensor_copy)
-            second = cast_half(e, 1, nc.scalar.copy)
-            quantize_half(e, 0, first)
-            quantize_half(e, 1, second)
+        def own(e):
+            return slice(e * C, (e + 1) * C)
 
-        def cast_side(e, side, grouped, copy):
-            half_m = P // 2
-            source = wa_cols[e, side][:].rearrange("p j (m u t) -> p u m j t", u=2, t=2)
-            target = grouped[:, :, side * half_m : (side + 1) * half_m, :].rearrange("p (u t) m j -> p u m j t", u=2)
-            copy(target, source)
-
-        def quantize_both(e, grouped):
-            for half in range(2):
-                quantize_half(e, half, grouped[:, 2 * half : 2 * half + 2, :, :])
-
-        def hidden(e, rounded, codes_tag):
-            bank = psum.tile([P, PACK, C], F32, name="h_bank%d" % e, tag="bank%d" % H_BANK[e])
-            for t in range(PACK):
-                cols = slice((t % 2) * P, (t % 2 + 1) * P)
+        def hidden(e, bank_tag, rounded, order):
+            bank = psum.tile([P, PACK, C], F32, name="h_bank%d" % e, tag=bank_tag)
+            for t in order:
+                cols = slice(t * P, (t + 1) * P)
                 nc.tensor.matmul_mx(
                     out=bank[:, t, :],
-                    lhsT=wa_codes[e, t // 2][:, cols].bitcast(FP8X4),
-                    lhsT_scale=wa_scales[e, t // 2][:, cols],
-                    rhs=slot_words[e],
-                    rhs_scale=slot_scales[e],
+                    lhsT=wa_codes[e][:, cols].bitcast(FP8X4),
+                    lhsT_scale=wa_scales[e][:, cols],
+                    rhs=words[:, own(e)].bitcast(FP8X4),
+                    rhs_scale=word_scales[:, own(e)],
                     start=True,
                     stop=True,
                 )
             nc.scalar.activation(rounded.rearrange("p (n t) -> p n t", t=PACK), bank[:].rearrange("p t n -> p n t"), GELU)
-            codes = keep.tile([P, C], U32, name="h_codes%d" % e, tag=codes_tag, align_bytes=ALIGN)
-            scales = keep.tile([P, C], U8, name="h_scales%d" % e, align_bytes=ALIGN)
-            nc.vector.quantize_mx(out=codes[:].bitcast(FP8X4), scales=scales[:], in_=rounded)
-            h_codes[e] = codes
-            h_scales[e] = scales
 
-        def product(e, r):
-            bank = psum.tile([P, 4 * C], F32, name="y_bank%d_%d" % (e, r), tag="bank%d" % Y_BANK[e][r])
-            cols = slice(r * P, (r + 1) * P)
-            nc.tensor.matmul_mx(
-                out=bank[:, 0:C],
-                lhsT=w_codes[e][:, 2 * r * P : 2 * (r + 1) * P].bitcast(FP4X4),
-                lhsT_scale=ws_plane[:, e, cols],
-                rhs=slot_words[e],
-                rhs_scale=slot_scales[e],
-                start=True,
-                stop=False,
-            )
-            nc.tensor.matmul_mx(
-                out=bank[:, 0:C],
-                lhsT=wb_codes[e][:, cols].bitcast(FP8X4),
-                lhsT_scale=wbs_plane[4 * e : P, cols],
-                rhs=h_codes[e][:].bitcast(FP8X4),
-                rhs_scale=h_scales[e][:],
-                start=False,
-                stop=True,
-            )
-            return bank
+        def quantize_hidden(e, rounded, codes_tag=None):
+            h_codes[e] = sb([P, C], U32, "h_codes%d" % e, codes_tag)
+            h_scales[e] = sb([P, C], U8, "h_scales%d" % e)
+            nc.vector.quantize_mx(out=h_codes[e][:].bitcast(FP8X4), scales=h_scales[e][:], in_=rounded)
+
+        def products(e, first, count, bank_tag):
+            bank = psum.tile([P, PACK * C], F32, name="y_bank%d_%d" % (e, first), tag=bank_tag)
+            for i in range(count):
+                r = first + i
+                cols = slice(r * P, (r + 1) * P)
+                nc.tensor.matmul_mx(
+                    out=bank[:, own(i)],
+                    lhsT=w_codes[e][:, 2 * r * P : 2 * (r + 1) * P].bitcast(FP4X4),
+                    lhsT_scale=ws_plane[:, e, cols],
+                    rhs=words[:, own(e)].bitcast(FP8X4),
+                    rhs_scale=word_scales[:, own(e)],
+                    start=True,
+                    stop=False,
+                )
+                nc.tensor.matmul_mx(
+                    out=bank[:, own(i)],
+                    lhsT=wb_codes[e][:, cols].bitcast(FP8X4),
+                    lhsT_scale=wbs_plane[4 * e : P, cols],
+                    rhs=h_codes[e][:].bitcast(FP8X4),
+                    rhs_scale=h_scales[e][:],
+                    start=False,
+                    stop=True,
+                )
+            banks[e, first] = bank[:, 0 : count * C]
 
         def scatter(r, first, last, values):
             cols = offsets[:, first * LIST_COLS : last * LIST_COLS]
             weights = first_gates[:] if first == 0 else later_gates[:, (first - 1) * C : (last - 1) * C]
             nc.vector.tensor_tensor(windows[r][:].indirect(cols), values, weights, MULT)
 
-        def room(name, tag, blocks):
-            return keep.tile([P, blocks * C], F32, name=name, tag=tag, align_bytes=ALIGN)
+        def room(name, blocks, tag=None):
+            return sb([P, blocks * C], F32, name, tag)
 
-        def send(blocks, staged):
-            for i, (e, r) in enumerate(blocks):
-                cols = slice(i * C, (i + 1) * C)
-                nc.scalar.copy(staged[:, cols], banks[e, r][:, 0:C])
-                scatter(r, e, e + 1, staged[:, cols])
-
-        def products(e):
-            for r in range(R):
-                banks[e, r] = product(e, r)
+        def send(e, first, count, staged):
+            nc.scalar.copy(staged, banks[e, first])
+            for i in range(count):
+                scatter(first + i, e, e + 1, staged[:, own(i)])
 
         def store(r):
             nc.sync.dma_start(out=out[r * P : (r + 1) * P, :], in_=windows[r][:])
 
-        grouped = {e: keep.tile([P, PACK, P, PACK], BF16, name="grouped%d" % e, tag="grouped%d" % e, align_bytes=ALIGN) for e in range(1, E)}
-        gather()
-        prepare(0)
-        for side in range(2):
-            cast_side(1, side, grouped[1], nc.vector.tensor_copy)
-        hidden(0, room("h0", "h0", 2)[:].bitcast(BF16), "raw1_1")
-        quantize_both(1, grouped[1])
-        products(0)
-        send([(0, 0), (0, 1), (0, 2)], room("early0", "early0", 3))
-        with_gelu = {1: [(0, 3)], 2: [(1, 2)]}
-        after_cast = {1: [(1, 0), (1, 1)], 2: [(1, 3), (2, 0)]}
-        for e in range(1, E - 1):
-            cast_side(e + 1, 0, grouped[e + 1], nc.scalar.copy)
-            shared = room("shared%d" % e, "raw%d_0" % (e + 1), 3)
-            hidden(e, shared[:, 0 : 2 * C].bitcast(BF16), "hc%d" % e)
-            send(with_gelu[e], shared[:, 2 * C :])
-            products(e)
-            cast_side(e + 1, 1, grouped[e + 1], nc.scalar.copy)
-            quantize_both(e + 1, grouped[e + 1])
-            send(after_cast[e], room("after%d" % e, "raw%d_1" % (e + 1), 2))
-        hidden(3, room("h3", "h3", 2)[:].bitcast(BF16), "hc3")
-        send([(2, 1), (2, 2)], room("late2", "wac3_1", 2))
-        last_rows = room("last_rows", "wac3_0", 2)
-        nc.scalar.copy(last_rows[:, 0:C], banks[2, 3][:, 0:C])
-        products(3)
+        def shared_cast(e, tag):
+            late = cast_pair(e, 1, nc.vector.tensor_copy)
+            early = cast_pair(e, 0, nc.scalar.copy, tag)
+            quantize_pair(e, 1, late)
+            quantize_pair(e, 0, early)
+
+        def scalar_cast(e, tag):
+            return [cast_pair(e, 0, nc.scalar.copy, tag), cast_pair(e, 1, nc.scalar.copy)]
+
+        def activate(e, bank_tag, order):
+            rounded = room("h%d" % e, 2)[:].bitcast(BF16)
+            hidden(e, bank_tag, rounded, order)
+            quantize_hidden(e, rounded)
+
+        shared_cast(0, None)
+        activate(0, "bank0", (2, 3, 0, 1))
+        shared_cast(1, "was0")
+        products(0, 0, 1, "bank1")
+        products(0, 1, 2, "bank2")
+        products(0, 3, 1, "bank3")
+        send(0, 0, 1, room("st00", 1)[:])
+        send(0, 1, 2, room("st01", 2)[:])
+        activate(1, "bank1", (2, 3, 0, 1))
+        send(0, 3, 1, room("st03", 1, "wac1")[:])
+        products(1, 0, 2, "bank4")
+        products(1, 2, 2, "bank5")
+        pairs = scalar_cast(2, "was1")
+        for u in range(2):
+            quantize_pair(2, u, pairs[u])
+        send(1, 0, 2, room("st10", 2, "raw2")[:])
+        activate(2, "bank0", (0, 1, 2, 3))
+        send(1, 2, 2, room("st12", 2, "wac2")[:])
+        products(2, 0, 2, "bank6")
+        products(2, 2, 2, "bank7")
+        pairs = scalar_cast(3, "was2")
+        for u in range(2):
+            quantize_pair(3, u, pairs[u])
+        send(2, 0, 2, room("st20", 2, "raw3")[:])
+        activate(3, "bank1", (0, 1, 2, 3))
+        last = room("st22", 3, "wac3")
+        nc.scalar.copy(last[:, 0 : 2 * C], banks[2, 2])
+        scatter(2, 2, 3, last[:, 0:C])
+        for r, tag in enumerate(("bank2", "bank3", "bank4", "bank0")):
+            products(3, r, 1, tag)
         for r in range(R - 1):
-            send([(3, r)], room("own3_%d" % r, "own3_%d" % r, 1))
+            send(3, r, 1, room("st3%d" % r, 1)[:])
             store(r)
-        nc.scalar.copy(last_rows[:, C : 2 * C], banks[3, 3][:, 0:C])
-        scatter(3, 2, 4, last_rows[:])
+        nc.scalar.copy(last[:, 2 * C :], banks[3, 3])
+        scatter(3, 2, 4, last[:, C:])
         store(3)

@@ -64,12 +64,12 @@ def tile_moe_elr_gelu_kernel(tc, x_words, x_scales, w_words, w_scales, wa, wb_wo
             nc.sync.dma_start(out=wb_codes[e][:], in_=wb_words[e, 0].rearrange("p n d -> p (n d)").bitcast(I32))
 
         def load_xs(q):
-            rows = x_scales[0, 4 * q : 4 * q + 4, :].bitcast(I32)
-            nc.sync.dma_start(out=xs_table[32 * q : 32 * q + 4, :].bitcast(I32), in_=rows)
+            rows = x_scales[0, q:16:4, :].bitcast(I32)
+            nc.sync.dma_start(out=xs_table[q:P:32, :].bitcast(I32), in_=rows)
 
         def load_ws(q):
-            rows = w_scales[:, 0, 4 * q : 4 * q + 4, :].bitcast(I32).rearrange("e b n -> b e n")
-            nc.sync.dma_start(out=ws_plane[32 * q : 32 * q + 4, :, :].bitcast(I32), in_=rows)
+            rows = w_scales[:, 0, q:16:4, :].bitcast(I32).rearrange("e b n -> b e n")
+            nc.sync.dma_start(out=ws_plane[q:P:32, :, :].bitcast(I32), in_=rows)
 
         def load_wbs(q):
             rows = wb_scales[:, 0, 4 * q : 4 * q + 4, :].bitcast(I32)

@@ -23,6 +23,7 @@ R = N // P
 LIST_COLS = C // 16
 ALIGN = 64
 HALF_M = P // 2
+SCALAR_M = 96
 
 
 def tile_moe_elr_gelu_kernel(tc, x_words, x_scales, w_words, w_scales, wa, wb_words, wb_scales, gate, offs, out):
@@ -116,10 +117,15 @@ def tile_moe_elr_gelu_kernel(tc, x_words, x_scales, w_words, w_scales, wa, wb_wo
             pair = sb([P, 2, P, PACK], BF16, "grouped%d_%d" % (e, u), tag)
             source = wa_raw[e][:].rearrange("p j (m t) -> p m j t", t=PACK)[:, :, :, 2 * u : 2 * u + 2]
             copy(pair[:].rearrange("p t m j -> p m j t"), source)
-            return pair
+            return pair[:]
 
         def quantize_pair(e, u, pair):
-            quantize(e, 2 * u * P, 2 * P, pair[:].rearrange("p t m j -> p (t m j)"))
+            quantize(e, 2 * u * P, 2 * P, pair.rearrange("p t m j -> p (t m j)"))
+
+        def cast_side(e, side, grouped):
+            source = wa_raw[e][:, :, side * H // 2 : (side + 1) * H // 2].rearrange("p j (m u t) -> p u m j t", u=2, t=2)
+            target = grouped[:, :, side * HALF_M : (side + 1) * HALF_M, :].rearrange("p (u t) m j -> p u m j t", u=2)
+            nc.scalar.copy(target, source)
 
         def own(e):
             return slice(e * C, (e + 1) * C)
@@ -185,14 +191,22 @@ def tile_moe_elr_gelu_kernel(tc, x_words, x_scales, w_words, w_scales, wa, wb_wo
         def store(r):
             nc.sync.dma_start(out=out[r * P : (r + 1) * P, :], in_=windows[r][:])
 
+        def split_pair(e, u, tag=None):
+            pair = sb([P, 2, P, PACK], BF16, "grouped%d_%d" % (e, u), tag)
+            source = wa_raw[e][:].rearrange("p j (m t) -> p m j t", t=PACK)[:, :, :, 2 * u : 2 * u + 2]
+            target = pair[:].rearrange("p t m j -> p m j t")
+            nc.scalar.copy(target[:, 0:SCALAR_M, :, :], source[:, 0:SCALAR_M, :, :])
+            nc.vector.tensor_copy(target[:, SCALAR_M:P, :, :], source[:, SCALAR_M:P, :, :])
+            return pair[:]
+
         def shared_cast(e, tag):
             late = cast_pair(e, 1, nc.vector.tensor_copy)
-            early = cast_pair(e, 0, nc.scalar.copy, tag)
+            early = split_pair(e, 0) if e == 0 else cast_pair(e, 0, nc.scalar.copy, tag)
             quantize_pair(e, 1, late)
             quantize_pair(e, 0, early)
 
         def scalar_cast(e, tag):
-            return [cast_pair(e, 0, nc.scalar.copy, tag), cast_pair(e, 1, nc.scalar.copy)]
+            return [cast_pair(e, 0, nc.scalar.copy, tag), split_pair(e, 1)]
 
         def activate(e, bank_tag, order):
             rounded = room("h%d" % e, 2)[:].bitcast(BF16)
@@ -209,20 +223,24 @@ def tile_moe_elr_gelu_kernel(tc, x_words, x_scales, w_words, w_scales, wa, wb_wo
         send(0, 1, 2, room("st01", 2)[:])
         activate(1, "bank1", (2, 3, 0, 1))
         send(0, 3, 1, room("st03", 1, "wac1")[:])
-        products(1, 0, 2, "bank4")
-        products(1, 2, 2, "bank5")
+        products(1, 0, 3, "bank4")
+        products(1, 3, 1, "bank5")
         pairs = scalar_cast(2, "was1")
         for u in range(2):
             quantize_pair(2, u, pairs[u])
-        send(1, 0, 2, room("st10", 2, "raw2")[:])
-        activate(2, "bank0", (0, 1, 2, 3))
-        send(1, 2, 2, room("st12", 2, "wac2")[:])
+        send(1, 0, 3, room("st10", 3, "raw2")[:])
+        grouped = sb([P, PACK, P, PACK], BF16, "grouped3")
+        cast_side(3, 0, grouped)
+        rounded = wa_raw[3][:, 0, 0 : H // 2].bitcast(BF16)
+        hidden(2, "bank0", rounded, (0, 1, 2, 3))
+        quantize_hidden(2, rounded)
+        send(1, 3, 1, wa_raw[3][:, 1, 0:C])
         products(2, 0, 2, "bank6")
         products(2, 2, 2, "bank7")
-        pairs = scalar_cast(3, "was2")
+        cast_side(3, 1, grouped)
         for u in range(2):
-            quantize_pair(3, u, pairs[u])
-        send(2, 0, 2, room("st20", 2, "raw3")[:])
+            quantize_pair(3, u, grouped[:, 2 * u : 2 * u + 2, :, :])
+        send(2, 0, 2, wa_raw[3][:, 0, H // 2 : H])
         activate(3, "bank1", (0, 1, 2, 3))
         last = room("st22", 3, "wac3")
         nc.scalar.copy(last[:, 0 : 2 * C], banks[2, 2])

@@ -1,6 +1,7 @@
 from contextlib import ExitStack
 
 import concourse.mybir as mybir
+from concourse.masks import make_identity
 
 K, T, E, C, H, N = 512, 1024, 4, 128, 512, 512
 FLOPS = 2 * E * C * (K * H + K * N + H * N)
@@ -40,8 +41,10 @@ def tile_moe_elr_gelu_kernel(tc, x_words, x_scales, w_words, w_scales, wa, wb_wo
         xs_table = sb([P, T], U8, "xs_table")
         ws_plane = sb([P, E, N], U8, "ws_plane")
         wbs_plane = sb([P, N], U8, "wbs_plane")
-        first_gates = sb([P, C], F32, "first_gates")
-        later_gates = sb([P, (E - 1) * C], F32, "later_gates")
+        gate_cols = sb([P, PACK], F32, "gate_cols")
+        gates = sb([P, E * C], F32, "gates")
+        identity = sb([P, P], F32, "identity")
+        make_identity(nc, identity[:])
         windows = [sb([P, T], F32, "window%d" % r) for r in range(R)]
         wa_raw = [sb([P, PACK, H], F32, "raw%d" % e) for e in range(E)]
         w_codes = [sb([P, 2 * N], U8, "w_codes%d" % e) for e in range(E)]
@@ -81,7 +84,7 @@ def tile_moe_elr_gelu_kernel(tc, x_words, x_scales, w_words, w_scales, wa, wb_wo
         for q in range(QUADS):
             load_xs(q)
         load_wa(0)
-        nc.sync.dma_start(out=first_gates[:], in_=gate[:, 0:C])
+        nc.sync.dma_start(out=gate_cols[:], in_=gate[0].rearrange("(p t) -> p t", t=PACK))
         for q in range(QUADS):
             load_ws(q)
         load_wa(1)
@@ -92,7 +95,6 @@ def tile_moe_elr_gelu_kernel(tc, x_words, x_scales, w_words, w_scales, wa, wb_wo
         load_wa(2)
         load_w(1)
         load_wb(1)
-        nc.sync.dma_start(out=later_gates[:], in_=gate[:, C : E * C])
         load_wa(3)
         for e in (2, 3):
             load_w(e)
@@ -177,7 +179,7 @@ def tile_moe_elr_gelu_kernel(tc, x_words, x_scales, w_words, w_scales, wa, wb_wo
 
         def scatter(r, first, last, values):
             cols = offsets[:, first * LIST_COLS : last * LIST_COLS]
-            weights = first_gates[:] if first == 0 else later_gates[:, (first - 1) * C : (last - 1) * C]
+            weights = gates[:, first * C : last * C]
             nc.vector.tensor_tensor(windows[r][:].indirect(cols), values, weights, MULT)
 
         def room(name, blocks, tag=None):
@@ -203,7 +205,8 @@ def tile_moe_elr_gelu_kernel(tc, x_words, x_scales, w_words, w_scales, wa, wb_wo
             late = cast_pair(e, 1, nc.vector.tensor_copy)
             early = split_pair(e, 0) if e == 0 else cast_pair(e, 0, nc.scalar.copy, tag)
             quantize_pair(e, 1, late)
-            quantize_pair(e, 0, early)
+            for t in range(2):
+                quantize(e, t * P, P, early[:, t, :, :].rearrange("p m j -> p (m j)"))
 
         def scalar_cast(e, tag):
             return [cast_pair(e, 0, nc.scalar.copy, tag), split_pair(e, 1)]
@@ -214,6 +217,10 @@ def tile_moe_elr_gelu_kernel(tc, x_words, x_scales, w_words, w_scales, wa, wb_wo
             quantize_hidden(e, rounded)
 
         shared_cast(0, None)
+        spread = psum.tile([P, PACK, P], F32, name="gate_bank", tag="bank7")
+        for t in range(PACK):
+            nc.tensor.transpose(spread[:, t, :], gate_cols[:, t : t + 1].to_broadcast([P, P]), identity[:])
+        nc.scalar.copy(gates[:].rearrange("p (n t) -> p n t", t=PACK), spread[:].rearrange("p t n -> p n t"))
         activate(0, "bank0", (2, 3, 0, 1))
         shared_cast(1, "was0")
         products(0, 0, 1, "bank1")
@@ -223,12 +230,15 @@ def tile_moe_elr_gelu_kernel(tc, x_words, x_scales, w_words, w_scales, wa, wb_wo
         send(0, 1, 2, room("st01", 2)[:])
         activate(1, "bank1", (2, 3, 0, 1))
         send(0, 3, 1, room("st03", 1, "wac1")[:])
-        products(1, 0, 3, "bank4")
-        products(1, 3, 1, "bank5")
+        products(1, 0, 1, "bank4")
+        products(1, 1, 2, "bank5")
+        products(1, 3, 1, "bank3")
         pairs = scalar_cast(2, "was1")
         for u in range(2):
             quantize_pair(2, u, pairs[u])
-        send(1, 0, 3, room("st10", 3, "raw2")[:])
+        staged = room("st10", 3, "raw2")
+        send(1, 0, 1, staged[:, 0:C])
+        send(1, 1, 2, staged[:, C:])
         grouped = sb([P, PACK, P, PACK], BF16, "grouped3")
         cast_side(3, 0, grouped)
         rounded = wa_raw[3][:, 0, 0 : H // 2].bitcast(BF16)
@@ -245,7 +255,7 @@ def tile_moe_elr_gelu_kernel(tc, x_words, x_scales, w_words, w_scales, wa, wb_wo
         last = room("st22", 3, "wac3")
         nc.scalar.copy(last[:, 0 : 2 * C], banks[2, 2])
         scatter(2, 2, 3, last[:, 0:C])
-        for r, tag in enumerate(("bank2", "bank3", "bank4", "bank0")):
+        for r, tag in enumerate(("bank2", "bank4", "bank5", "bank0")):
             products(3, r, 1, tag)
         for r in range(R - 1):
             send(3, r, 1, room("st3%d" % r, 1)[:])

@@ -129,6 +129,11 @@ def tile_moe_elr_gelu_kernel(tc, x_words, x_scales, w_words, w_scales, wa, wb_wo
             target = grouped[:, :, side * HALF_M : (side + 1) * HALF_M, :].rearrange("p (u t) m j -> p u m j t", u=2)
             nc.scalar.copy(target, source)
 
+        def cast_side_pair(e, side, u, grouped):
+            source = wa_raw[e][:, :, side * H // 2 : (side + 1) * H // 2].rearrange("p j (m t) -> p m j t", t=PACK)
+            target = grouped[:, 2 * u : 2 * u + 2, side * HALF_M : (side + 1) * HALF_M, :].rearrange("p t m j -> p m j t")
+            nc.scalar.copy(target, source[:, :, :, 2 * u : 2 * u + 2])
+
         def own(e):
             return slice(e * C, (e + 1) * C)
 
@@ -244,22 +249,25 @@ def tile_moe_elr_gelu_kernel(tc, x_words, x_scales, w_words, w_scales, wa, wb_wo
         rounded = wa_raw[3][:, 0, 0 : H // 2].bitcast(BF16)
         hidden(2, "bank0", rounded, (0, 1, 2, 3))
         quantize_hidden(2, rounded)
-        send(1, 3, 1, wa_raw[3][:, 1, 0:C])
-        products(2, 0, 2, "bank6")
-        products(2, 2, 2, "bank7")
-        cast_side(3, 1, grouped)
+        for u in range(2):
+            cast_side_pair(3, 1, u, grouped)
         for u in range(2):
             quantize_pair(3, u, grouped[:, 2 * u : 2 * u + 2, :, :])
-        send(2, 0, 2, wa_raw[3][:, 0, H // 2 : H])
+        send(1, 3, 1, wa_raw[3][:, 1, H // 2 : H // 2 + C])
+        products(2, 0, 1, "bank6")
+        send(2, 0, 1, wa_raw[3][:, 0, H // 2 : H // 2 + C])
         activate(3, "bank1", (0, 1, 2, 3))
-        last = room("st22", 3, "wac3")
-        nc.scalar.copy(last[:, 0 : 2 * C], banks[2, 2])
-        scatter(2, 2, 3, last[:, 0:C])
+        last = room("st21", 4, "wac3")
+        products(2, 1, 1, "bank6")
+        products(2, 2, 2, "bank3")
+        send(2, 1, 1, last[:, 0:C])
+        nc.scalar.copy(last[:, C : 3 * C], banks[2, 2])
+        scatter(2, 2, 3, last[:, C : 2 * C])
         for r, tag in enumerate(("bank2", "bank4", "bank5", "bank0")):
             products(3, r, 1, tag)
         for r in range(R - 1):
             send(3, r, 1, room("st3%d" % r, 1)[:])
             store(r)
-        nc.scalar.copy(last[:, 2 * C :], banks[3, 3])
-        scatter(3, 2, 4, last[:, C:])
+        nc.scalar.copy(last[:, 3 * C :], banks[3, 3])
+        scatter(3, 2, 4, last[:, 2 * C :])
         store(3)

@@ -25,6 +25,7 @@ LIST_COLS = C // 16
 ALIGN = 64
 HALF_M = P // 2
 SCALAR_M = 96
+LAST_M = 112
 
 
 def tile_moe_elr_gelu_kernel(tc, x_words, x_scales, w_words, w_scales, wa, wb_words, wb_scales, gate, offs, out):
@@ -71,9 +72,9 @@ def tile_moe_elr_gelu_kernel(tc, x_words, x_scales, w_words, w_scales, wa, wb_wo
             rows = x_scales[0, q:16:4, :].bitcast(I32)
             nc.sync.dma_start(out=xs_table[q:P:32, :].bitcast(I32), in_=rows)
 
-        def load_ws(q):
-            rows = w_scales[:, 0, q:16:4, :].bitcast(I32).rearrange("e b n -> b e n")
-            nc.sync.dma_start(out=ws_plane[q:P:32, :, :].bitcast(I32), in_=rows)
+        def load_ws(q, first):
+            rows = w_scales[first : first + 2, 0, q:16:4, :].bitcast(I32).rearrange("e b n -> b e n")
+            nc.sync.dma_start(out=ws_plane[q:P:32, first : first + 2, :].bitcast(I32), in_=rows)
 
         def load_wbs(q):
             rows = wb_scales[:, 0, 4 * q : 4 * q + 4, :].bitcast(I32)
@@ -86,13 +87,15 @@ def tile_moe_elr_gelu_kernel(tc, x_words, x_scales, w_words, w_scales, wa, wb_wo
         load_wa(0)
         nc.sync.dma_start(out=gate_cols[:], in_=gate[0].rearrange("(p t) -> p t", t=PACK))
         for q in range(QUADS):
-            load_ws(q)
+            load_ws(q, 0)
         load_wa(1)
         load_w(0)
         load_wb(0)
         for q in range(QUADS):
             load_wbs(q)
         load_wa(2)
+        for q in range(QUADS):
+            load_ws(q, 2)
         load_w(1)
         load_wb(1)
         load_wa(3)
@@ -129,10 +132,9 @@ def tile_moe_elr_gelu_kernel(tc, x_words, x_scales, w_words, w_scales, wa, wb_wo
             target = grouped[:, :, side * HALF_M : (side + 1) * HALF_M, :].rearrange("p (u t) m j -> p u m j t", u=2)
             nc.scalar.copy(target, source)
 
-        def cast_side_pair(e, side, u, grouped):
-            source = wa_raw[e][:, :, side * H // 2 : (side + 1) * H // 2].rearrange("p j (m t) -> p m j t", t=PACK)
-            target = grouped[:, 2 * u : 2 * u + 2, side * HALF_M : (side + 1) * HALF_M, :].rearrange("p t m j -> p m j t")
-            nc.scalar.copy(target, source[:, :, :, 2 * u : 2 * u + 2])
+        def cast_rows(e, u, first, last, grouped, copy):
+            source = wa_raw[e][:].rearrange("p j (m t) -> p m j t", t=PACK)[:, first:last, :, 2 * u : 2 * u + 2]
+            copy(grouped[:, 2 * u : 2 * u + 2, first:last, :].rearrange("p t m j -> p m j t"), source)
 
         def own(e):
             return slice(e * C, (e + 1) * C)
@@ -247,12 +249,14 @@ def tile_moe_elr_gelu_kernel(tc, x_words, x_scales, w_words, w_scales, wa, wb_wo
         grouped = sb([P, PACK, P, PACK], BF16, "grouped3")
         cast_side(3, 0, grouped)
         rounded = wa_raw[3][:, 0, 0 : H // 2].bitcast(BF16)
-        hidden(2, "bank0", rounded, (0, 1, 2, 3))
+        hidden(2, "bank4", rounded, (0, 1, 2, 3))
         quantize_hidden(2, rounded)
-        for u in range(2):
-            cast_side_pair(3, 1, u, grouped)
-        for u in range(2):
-            quantize_pair(3, u, grouped[:, 2 * u : 2 * u + 2, :, :])
+        cast_rows(3, 1, LAST_M, P, grouped, nc.vector.tensor_copy)
+        cast_rows(3, 0, HALF_M, P, grouped, nc.scalar.copy)
+        cast_rows(3, 1, HALF_M, LAST_M, grouped, nc.scalar.copy)
+        quantize_pair(3, 0, grouped[:, 0:2, :, :])
+        for t in (2, 3):
+            quantize(3, t * P, P, grouped[:, t, :, :].rearrange("p m j -> p (m j)"))
         send(1, 3, 1, wa_raw[3][:, 1, H // 2 : H // 2 + C])
         products(2, 0, 1, "bank6")
         send(2, 0, 1, wa_raw[3][:, 0, H // 2 : H // 2 + C])

@@ -25,7 +25,6 @@ LIST_COLS = C // 16
 ALIGN = 64
 HALF_M = P // 2
 SCALAR_M = 96
-LAST_M = 112
 
 
 def tile_moe_elr_gelu_kernel(tc, x_words, x_scales, w_words, w_scales, wa, wb_words, wb_scales, gate, offs, out):
@@ -72,9 +71,10 @@ def tile_moe_elr_gelu_kernel(tc, x_words, x_scales, w_words, w_scales, wa, wb_wo
             rows = x_scales[0, q:16:4, :].bitcast(I32)
             nc.sync.dma_start(out=xs_table[q:P:32, :].bitcast(I32), in_=rows)
 
-        def load_ws(q, first):
-            rows = w_scales[first : first + 2, 0, q:16:4, :].bitcast(I32).rearrange("e b n -> b e n")
-            nc.sync.dma_start(out=ws_plane[q:P:32, first : first + 2, :].bitcast(I32), in_=rows)
+        def load_ws(first, last):
+            for q in range(QUADS):
+                rows = w_scales[first:last, 0, q:16:4, :].bitcast(I32).rearrange("e b n -> b e n")
+                nc.sync.dma_start(out=ws_plane[q:P:32, first:last, :].bitcast(I32), in_=rows)
 
         def load_wbs(q):
             rows = wb_scales[:, 0, 4 * q : 4 * q + 4, :].bitcast(I32)
@@ -86,22 +86,22 @@ def tile_moe_elr_gelu_kernel(tc, x_words, x_scales, w_words, w_scales, wa, wb_wo
             load_xs(q)
         load_wa(0)
         nc.sync.dma_start(out=gate_cols[:], in_=gate[0].rearrange("(p t) -> p t", t=PACK))
-        for q in range(QUADS):
-            load_ws(q, 0)
+        load_ws(0, 1)
         load_wa(1)
         load_w(0)
         load_wb(0)
         for q in range(QUADS):
             load_wbs(q)
         load_wa(2)
-        for q in range(QUADS):
-            load_ws(q, 2)
+        load_ws(1, 3)
         load_w(1)
         load_wb(1)
         load_wa(3)
-        for e in (2, 3):
-            load_w(e)
-            load_wb(e)
+        load_w(2)
+        load_wb(2)
+        load_ws(3, 4)
+        load_w(3)
+        load_wb(3)
 
         words = sb([P, E * C], U32, "slot_words")
         word_scales = sb([P, E * C], U8, "slot_scales")
@@ -114,9 +114,12 @@ def tile_moe_elr_gelu_kernel(tc, x_words, x_scales, w_words, w_scales, wa, wb_wo
         h_scales = {}
         banks = {}
 
+        def wa_plane(e, first, count):
+            return wa_scales[e][:, first : first + count]
+
         def quantize(e, first, count, values):
-            cols = slice(first, first + count)
-            nc.vector.quantize_mx(out=wa_codes[e][:, cols].bitcast(FP8X4), scales=wa_scales[e][:, cols], in_=values)
+            codes = wa_codes[e][:, first : first + count].bitcast(FP8X4)
+            nc.vector.quantize_mx(out=codes, scales=wa_plane(e, first, count), in_=values)
 
         def cast_pair(e, u, copy, tag=None):
             pair = sb([P, 2, P, PACK], BF16, "grouped%d_%d" % (e, u), tag)
@@ -146,7 +149,7 @@ def tile_moe_elr_gelu_kernel(tc, x_words, x_scales, w_words, w_scales, wa, wb_wo
                 nc.tensor.matmul_mx(
                     out=bank[:, t, :],
                     lhsT=wa_codes[e][:, cols].bitcast(FP8X4),
-                    lhsT_scale=wa_scales[e][:, cols],
+                    lhsT_scale=wa_plane(e, t * P, P),
                     rhs=words[:, own(e)].bitcast(FP8X4),
                     rhs_scale=word_scales[:, own(e)],
                     start=True,
@@ -154,35 +157,45 @@ def tile_moe_elr_gelu_kernel(tc, x_words, x_scales, w_words, w_scales, wa, wb_wo
                 )
             nc.scalar.activation(rounded.rearrange("p (n t) -> p n t", t=PACK), bank[:].rearrange("p t n -> p n t"), GELU)
 
-        def quantize_hidden(e, rounded, codes_tag=None):
-            h_codes[e] = sb([P, C], U32, "h_codes%d" % e, codes_tag)
-            h_scales[e] = sb([P, C], U8, "h_scales%d" % e)
-            nc.vector.quantize_mx(out=h_codes[e][:].bitcast(FP8X4), scales=h_scales[e][:], in_=rounded)
+        def quantize_hidden(e, rounded, scales=None):
+            h_codes[e] = sb([P, C], U32, "h_codes%d" % e)
+            h_scales[e] = sb([P, C], U8, "h_scales%d" % e)[:] if scales is None else scales
+            nc.vector.quantize_mx(out=h_codes[e][:].bitcast(FP8X4), scales=h_scales[e], in_=rounded)
+
+        def frozen(e, r, sums):
+            nc.tensor.matmul_mx(
+                out=sums,
+                lhsT=w_codes[e][:, 2 * r * P : 2 * (r + 1) * P].bitcast(FP4X4),
+                lhsT_scale=ws_plane[:, e, r * P : (r + 1) * P],
+                rhs=words[:, own(e)].bitcast(FP8X4),
+                rhs_scale=word_scales[:, own(e)],
+                start=True,
+                stop=False,
+            )
+
+        def adapter(e, r, sums):
+            cols = slice(r * P, (r + 1) * P)
+            nc.tensor.matmul_mx(
+                out=sums,
+                lhsT=wb_codes[e][:, cols].bitcast(FP8X4),
+                lhsT_scale=wbs_plane[4 * e : P, cols],
+                rhs=h_codes[e][:].bitcast(FP8X4),
+                rhs_scale=h_scales[e],
+                start=False,
+                stop=True,
+            )
 
         def products(e, first, count, bank_tag):
             bank = psum.tile([P, PACK * C], F32, name="y_bank%d_%d" % (e, first), tag=bank_tag)
             for i in range(count):
-                r = first + i
-                cols = slice(r * P, (r + 1) * P)
-                nc.tensor.matmul_mx(
-                    out=bank[:, own(i)],
-                    lhsT=w_codes[e][:, 2 * r * P : 2 * (r + 1) * P].bitcast(FP4X4),
-                    lhsT_scale=ws_plane[:, e, cols],
-                    rhs=words[:, own(e)].bitcast(FP8X4),
-                    rhs_scale=word_scales[:, own(e)],
-                    start=True,
-                    stop=False,
-                )
-                nc.tensor.matmul_mx(
-                    out=bank[:, own(i)],
-                    lhsT=wb_codes[e][:, cols].bitcast(FP8X4),
-                    lhsT_scale=wbs_plane[4 * e : P, cols],
-                    rhs=h_codes[e][:].bitcast(FP8X4),
-                    rhs_scale=h_scales[e][:],
-                    start=False,
-                    stop=True,
-                )
+                frozen(e, first + i, bank[:, own(i)])
+                adapter(e, first + i, bank[:, own(i)])
             banks[e, first] = bank[:, 0 : count * C]
+
+        def open_block(e, r, bank_tag):
+            bank = psum.tile([P, PACK * C], F32, name="y_bank%d_%d" % (e, r), tag=bank_tag)
+            banks[e, r] = bank[:, 0:C]
+            frozen(e, r, banks[e, r])
 
         def scatter(r, first, last, values):
             cols = offsets[:, first * LIST_COLS : last * LIST_COLS]
@@ -228,37 +241,51 @@ def tile_moe_elr_gelu_kernel(tc, x_words, x_scales, w_words, w_scales, wa, wb_wo
         for t in range(PACK):
             nc.tensor.transpose(spread[:, t, :], gate_cols[:, t : t + 1].to_broadcast([P, P]), identity[:])
         nc.scalar.copy(gates[:].rearrange("p (n t) -> p n t", t=PACK), spread[:].rearrange("p t n -> p n t"))
-        activate(0, "bank0", (2, 3, 0, 1))
-        shared_cast(1, "was0")
-        products(0, 0, 1, "bank1")
-        products(0, 1, 2, "bank2")
-        products(0, 3, 1, "bank3")
+        rounded = room("h0", 2)[:].bitcast(BF16)
+        hidden(0, "bank0", rounded, (2, 3, 0, 1))
+        grouped = sb([P, PACK, P, PACK], BF16, "grouped1")
+        tail = wa_raw[1][:, :, PACK * SCALAR_M : H].rearrange("p j (m u t) -> p u m j t", u=2, t=2)
+        nc.vector.tensor_copy(grouped[:, :, SCALAR_M:P, :].rearrange("p (u t) m j -> p u m j t", u=2), tail)
+        cast_rows(1, 1, 0, SCALAR_M, grouped, nc.vector.tensor_copy)
+        for r, tag in enumerate(("bank1", "bank2", "bank4", "bank3")):
+            open_block(0, r, tag)
+        quantize_hidden(0, rounded, ws_plane[:, 0, 0:C])
+        cast_rows(1, 0, 0, SCALAR_M, grouped, nc.scalar.copy)
+        quantize_pair(1, 1, grouped[:, 2:4, :, :])
+        for t in range(2):
+            quantize(1, t * P, P, grouped[:, t, :, :].rearrange("p m j -> p (m j)"))
+        for r in range(R):
+            adapter(0, r, banks[0, r])
         send(0, 0, 1, room("st00", 1)[:])
-        send(0, 1, 2, room("st01", 2)[:])
-        activate(1, "bank1", (2, 3, 0, 1))
+        for r in (1, 2):
+            send(0, r, 1, room("st0%d" % r, 1)[:])
+        rounded = room("h1", 2)[:].bitcast(BF16)
+        hidden(1, "bank1", rounded, (2, 3, 0, 1))
         send(0, 3, 1, room("st03", 1, "wac1")[:])
-        products(1, 0, 1, "bank4")
-        products(1, 1, 2, "bank5")
-        products(1, 3, 1, "bank3")
+        for r, tag in enumerate(("bank4", "bank5", "bank0", "bank3")):
+            open_block(1, r, tag)
+        quantize_hidden(1, rounded)
+        for r in range(R):
+            adapter(1, r, banks[1, r])
         pairs = scalar_cast(2, "was1")
         for u in range(2):
             quantize_pair(2, u, pairs[u])
         staged = room("st10", 3, "raw2")
-        send(1, 0, 1, staged[:, 0:C])
-        send(1, 1, 2, staged[:, C:])
+        for r in range(R - 1):
+            send(1, r, 1, staged[:, own(r)])
         grouped = sb([P, PACK, P, PACK], BF16, "grouped3")
         cast_side(3, 0, grouped)
         rounded = wa_raw[3][:, 0, 0 : H // 2].bitcast(BF16)
         hidden(2, "bank4", rounded, (0, 1, 2, 3))
         quantize_hidden(2, rounded)
-        cast_rows(3, 1, LAST_M, P, grouped, nc.vector.tensor_copy)
-        cast_rows(3, 0, HALF_M, P, grouped, nc.scalar.copy)
-        cast_rows(3, 1, HALF_M, LAST_M, grouped, nc.scalar.copy)
+        open_block(2, 0, "bank6")
+        adapter(2, 0, banks[2, 0])
+        for u in range(2):
+            cast_rows(3, u, HALF_M, P, grouped, nc.scalar.copy)
         quantize_pair(3, 0, grouped[:, 0:2, :, :])
         for t in (2, 3):
             quantize(3, t * P, P, grouped[:, t, :, :].rearrange("p m j -> p (m j)"))
         send(1, 3, 1, wa_raw[3][:, 1, H // 2 : H // 2 + C])
-        products(2, 0, 1, "bank6")
         send(2, 0, 1, wa_raw[3][:, 0, H // 2 : H // 2 + C])
         activate(3, "bank1", (0, 1, 2, 3))
         last = room("st21", 4, "wac3")

@@ -256,49 +256,62 @@ def tile_moe_elr_gelu_kernel(tc, x_words, x_scales, w_words, w_scales, wa, wb_wo
             quantize(1, t * P, P, grouped[:, t, :, :].rearrange("p m j -> p (m j)"))
         for r in range(R):
             adapter(0, r, banks[0, r])
-        send(0, 0, 1, room("st00", 1)[:])
-        for r in (1, 2):
+        for r in range(2):
             send(0, r, 1, room("st0%d" % r, 1)[:])
         rounded = room("h1", 2)[:].bitcast(BF16)
         hidden(1, "bank1", rounded, (2, 3, 0, 1))
-        send(0, 3, 1, room("st03", 1, "wac1")[:])
-        for r, tag in enumerate(("bank4", "bank5", "bank0", "bank3")):
+        staged = room("st02", 2, "wac1")
+        for i in range(2):
+            send(0, 2 + i, 1, staged[:, own(i)])
+        for r, tag in enumerate(("bank5", "bank6", "bank0", "bank7")):
             open_block(1, r, tag)
         quantize_hidden(1, rounded)
         for r in range(R):
             adapter(1, r, banks[1, r])
-        pairs = scalar_cast(2, "was1")
-        for u in range(2):
-            quantize_pair(2, u, pairs[u])
-        staged = room("st10", 3, "raw2")
-        for r in range(R - 1):
-            send(1, r, 1, staged[:, own(r)])
+
+        def spent(e, row, side):
+            return wa_raw[e][:, row, side * H // 2 : side * H // 2 + C]
+
+        def finish(e, grouped):
+            for u in range(2):
+                cast_rows(e, u, HALF_M, P, grouped, nc.scalar.copy)
+            quantize_pair(e, 0, grouped[:, 0:2, :, :])
+            for t in (2, 3):
+                quantize(e, t * P, P, grouped[:, t, :, :].rearrange("p m j -> p (m j)"))
+
+        grouped = sb([P, PACK, P, PACK], BF16, "grouped2", "was1")
+        cast_side(2, 0, grouped)
+        send(1, 0, 1, spent(2, 0, 0))
+        finish(2, grouped)
+        for r in (1, 2):
+            send(1, r, 1, spent(2, r, 1))
         grouped = sb([P, PACK, P, PACK], BF16, "grouped3")
         cast_side(3, 0, grouped)
         rounded = wa_raw[3][:, 0, 0 : H // 2].bitcast(BF16)
-        hidden(2, "bank4", rounded, (0, 1, 2, 3))
+        hidden(2, "bank5", rounded, (0, 1, 2, 3))
+        send(1, 3, 1, spent(3, 1, 0))
+        for r, tag in enumerate(("bank2", "bank4")):
+            open_block(2, r, tag)
         quantize_hidden(2, rounded)
-        open_block(2, 0, "bank6")
-        adapter(2, 0, banks[2, 0])
-        for u in range(2):
-            cast_rows(3, u, HALF_M, P, grouped, nc.scalar.copy)
-        quantize_pair(3, 0, grouped[:, 0:2, :, :])
-        for t in (2, 3):
-            quantize(3, t * P, P, grouped[:, t, :, :].rearrange("p m j -> p (m j)"))
-        send(1, 3, 1, wa_raw[3][:, 1, H // 2 : H // 2 + C])
-        send(2, 0, 1, wa_raw[3][:, 0, H // 2 : H // 2 + C])
-        activate(3, "bank1", (0, 1, 2, 3))
-        last = room("st21", 4, "wac3")
-        products(2, 1, 1, "bank6")
+        for r in range(2):
+            adapter(2, r, banks[2, r])
         products(2, 2, 2, "bank3")
-        send(2, 1, 1, last[:, 0:C])
-        nc.scalar.copy(last[:, C : 3 * C], banks[2, 2])
-        scatter(2, 2, 3, last[:, C : 2 * C])
-        for r, tag in enumerate(("bank2", "bank4", "bank5", "bank0")):
-            products(3, r, 1, tag)
+        finish(3, grouped)
+        for r in range(2):
+            send(2, r, 1, spent(3, r, 1))
+        rounded = room("h3", 2)[:].bitcast(BF16)
+        hidden(3, "bank1", rounded, (0, 1, 2, 3))
+        last = room("st22", 3, "wac3")
+        nc.scalar.copy(last[:, 0 : 2 * C], banks[2, 2])
+        scatter(2, 2, 3, last[:, 0:C])
+        for r, tag in enumerate(("bank5", "bank6", "bank0", "bank7")):
+            open_block(3, r, tag)
+        quantize_hidden(3, rounded)
+        for r in range(R):
+            adapter(3, r, banks[3, r])
         for r in range(R - 1):
             send(3, r, 1, room("st3%d" % r, 1)[:])
             store(r)
-        nc.scalar.copy(last[:, 3 * C :], banks[3, 3])
-        scatter(3, 2, 4, last[:, 2 * C :])
+        nc.scalar.copy(last[:, 2 * C :], banks[3, 3])
+        scatter(3, 2, 4, last[:, C:])
         store(3)

@@ -272,9 +272,11 @@ def tile_moe_elr_gelu_kernel(tc, x_words, x_scales, w_words, w_scales, wa, wb_wo
         def spent(e, row, side):
             return wa_raw[e][:, row, side * H // 2 : side * H // 2 + C]
 
-        def finish(e, grouped):
-            for u in range(2):
-                cast_rows(e, u, HALF_M, P, grouped, nc.scalar.copy)
+        def finish(e, grouped, last):
+            cast_rows(e, 0, HALF_M, P, grouped, nc.scalar.copy)
+            cast_rows(e, 1, HALF_M, last, grouped, nc.scalar.copy)
+            if last < P:
+                cast_rows(e, 1, last, P, grouped, nc.vector.tensor_copy)
             quantize_pair(e, 0, grouped[:, 0:2, :, :])
             for t in (2, 3):
                 quantize(e, t * P, P, grouped[:, t, :, :].rearrange("p m j -> p (m j)"))
@@ -282,29 +284,28 @@ def tile_moe_elr_gelu_kernel(tc, x_words, x_scales, w_words, w_scales, wa, wb_wo
         grouped = sb([P, PACK, P, PACK], BF16, "grouped2", "was1")
         cast_side(2, 0, grouped)
         send(1, 0, 1, spent(2, 0, 0))
-        finish(2, grouped)
+        finish(2, grouped, P)
         for r in (1, 2):
             send(1, r, 1, spent(2, r, 1))
         grouped = sb([P, PACK, P, PACK], BF16, "grouped3")
         cast_side(3, 0, grouped)
         rounded = wa_raw[3][:, 0, 0 : H // 2].bitcast(BF16)
         hidden(2, "bank5", rounded, (0, 1, 2, 3))
-        send(1, 3, 1, spent(3, 1, 0))
-        for r, tag in enumerate(("bank2", "bank4")):
-            open_block(2, r, tag)
+        open_block(2, 0, "bank2")
         quantize_hidden(2, rounded)
-        for r in range(2):
-            adapter(2, r, banks[2, r])
-        products(2, 2, 2, "bank3")
-        finish(3, grouped)
-        for r in range(2):
-            send(2, r, 1, spent(3, r, 1))
+        adapter(2, 0, banks[2, 0])
+        finish(3, grouped, P)
+        send(1, 3, 1, spent(3, 1, 1))
+        send(2, 0, 1, spent(3, 0, 1))
         rounded = room("h3", 2)[:].bitcast(BF16)
         hidden(3, "bank1", rounded, (0, 1, 2, 3))
-        last = room("st22", 3, "wac3")
-        nc.scalar.copy(last[:, 0 : 2 * C], banks[2, 2])
-        scatter(2, 2, 3, last[:, 0:C])
-        for r, tag in enumerate(("bank5", "bank6", "bank0", "bank7")):
+        last = room("st21", 4, "wac3")
+        products(2, 1, 1, "bank2")
+        products(2, 2, 2, "bank7")
+        send(2, 1, 1, last[:, 0:C])
+        nc.scalar.copy(last[:, C : 3 * C], banks[2, 2])
+        scatter(2, 2, 3, last[:, C : 2 * C])
+        for r, tag in enumerate(("bank5", "bank6", "bank0", "bank3")):
             open_block(3, r, tag)
         quantize_hidden(3, rounded)
         for r in range(R):
@@ -312,6 +313,6 @@ def tile_moe_elr_gelu_kernel(tc, x_words, x_scales, w_words, w_scales, wa, wb_wo
         for r in range(R - 1):
             send(3, r, 1, room("st3%d" % r, 1)[:])
             store(r)
-        nc.scalar.copy(last[:, 2 * C :], banks[3, 3])
-        scatter(3, 2, 4, last[:, C:])
+        nc.scalar.copy(last[:, 3 * C :], banks[3, 3])
+        scatter(3, 2, 4, last[:, 2 * C :])
         store(3)

@@ -131,8 +131,8 @@ def tile_moe_elr_gelu_kernel(tc, x_words, x_scales, w_words, w_scales, wa, wb_wo
             quantize(e, 2 * u * P, 2 * P, pair.rearrange("p t m j -> p (t m j)"))
 
         def cast_side(e, side, grouped):
-            source = wa_raw[e][:, :, side * H // 2 : (side + 1) * H // 2].rearrange("p j (m u t) -> p u m j t", u=2, t=2)
-            target = grouped[:, :, side * HALF_M : (side + 1) * HALF_M, :].rearrange("p (u t) m j -> p u m j t", u=2)
+            source = wa_raw[e][:, :, side * H // 2 : (side + 1) * H // 2].rearrange("p j (m t) -> p m j t", t=PACK)
+            target = grouped[:, :, side * HALF_M : (side + 1) * HALF_M, :].rearrange("p t m j -> p m j t")
             nc.scalar.copy(target, source)
 
         def cast_rows(e, u, first, last, grouped, copy):

@@ -15,6 +15,7 @@ U8 = mybir.dt.uint8
 FP8X4 = mybir.dt.float8_e4m3fn_x4
 FP4X4 = mybir.dt.float4_e2m1fn_x4
 GELU = mybir.ActivationFunctionType.Gelu_apprx_tanh
+COPY = mybir.ActivationFunctionType.Copy
 MULT = mybir.AluOpType.mult
 
 P = 128
@@ -23,7 +24,6 @@ QUADS = 4
 R = N // P
 LIST_COLS = C // 16
 ALIGN = 64
-HALF_M = P // 2
 SCALAR_M = 96
 
 
@@ -47,8 +47,8 @@ def tile_moe_elr_gelu_kernel(tc, x_words, x_scales, w_words, w_scales, wa, wb_wo
         make_identity(nc, identity[:])
         windows = [sb([P, T], F32, "window%d" % r) for r in range(R)]
         wa_raw = [sb([P, PACK, H], F32, "raw%d" % e) for e in range(E)]
-        w_codes = [sb([P, 2 * N], U8, "w_codes%d" % e) for e in range(E)]
-        wb_codes = [sb([P, N], I32, "wb_codes%d" % e) for e in range(E)]
+        w_codes = {}
+        wb_codes = {}
 
         nc.vector.memset(xs_table[:].bitcast(I32), 0)
         nc.vector.memset(windows[0][:], 0.0)
@@ -61,11 +61,19 @@ def tile_moe_elr_gelu_kernel(tc, x_words, x_scales, w_words, w_scales, wa, wb_wo
         def load_wa(e):
             nc.sync.dma_start(out=wa_raw[e][:], in_=wa[e].rearrange("(p j) c -> p j c", j=PACK))
 
-        def load_w(e):
-            nc.sync.dma_start(out=w_codes[e][:].bitcast(I32), in_=w_words[e, 0].bitcast(I32))
+        def load_w(first, last):
+            codes = sb([P, last - first, 2 * N], U8, "w_codes%d" % first)
+            rows = w_words[first:last, 0].bitcast(I32).rearrange("e p n -> p e n")
+            nc.sync.dma_start(out=codes[:].bitcast(I32), in_=rows)
+            for e in range(first, last):
+                w_codes[e] = codes[:, e - first, :]
 
-        def load_wb(e):
-            nc.sync.dma_start(out=wb_codes[e][:], in_=wb_words[e, 0].rearrange("p n d -> p (n d)").bitcast(I32))
+        def load_wb(first, last):
+            codes = sb([P, last - first, N], I32, "wb_codes%d" % first)
+            rows = wb_words[first:last, 0].rearrange("e p n d -> p e (n d)").bitcast(I32)
+            nc.sync.dma_start(out=codes[:], in_=rows)
+            for e in range(first, last):
+                wb_codes[e] = codes[:, e - first, :]
 
         def load_xs(q):
             rows = x_scales[0, q:16:4, :].bitcast(I32)
@@ -80,28 +88,32 @@ def tile_moe_elr_gelu_kernel(tc, x_words, x_scales, w_words, w_scales, wa, wb_wo
             rows = wb_scales[:, 0, 4 * q : 4 * q + 4, :].bitcast(I32)
             nc.sync.dma_start(out=wbs_plane[32 * q : 32 * q + 16, :].bitcast(I32), in_=rows)
 
-        nc.sync.dma_start(out=x_table[:], in_=x_words[0].rearrange("p t d -> p (t d)").bitcast(I32))
+        def load_x():
+            nc.sync.dma_start(out=x_table[:], in_=x_words[0].rearrange("p t d -> p (t d)").bitcast(I32))
+
+        def load_gate():
+            nc.sync.dma_start(out=gate_cols[:], in_=gate[0].rearrange("(p t) -> p t", t=PACK))
+
+        load_x()
         nc.sync.dma_start(offsets[:], offs)
         for q in range(QUADS):
             load_xs(q)
         load_wa(0)
-        nc.sync.dma_start(out=gate_cols[:], in_=gate[0].rearrange("(p t) -> p t", t=PACK))
-        load_ws(0, 1)
+        load_gate()
+        load_ws(0, 2)
         load_wa(1)
-        load_w(0)
-        load_wb(0)
+        load_w(0, 1)
+        load_wb(0, 1)
         for q in range(QUADS):
             load_wbs(q)
         load_wa(2)
-        load_ws(1, 3)
-        load_w(1)
-        load_wb(1)
+        load_w(1, 2)
+        load_wb(1, 2)
         load_wa(3)
-        load_w(2)
-        load_wb(2)
-        load_ws(3, 4)
-        load_w(3)
-        load_wb(3)
+        load_ws(2, 4)
+        load_w(2, 4)
+        load_wb(2, 3)
+        load_wb(3, 4)
 
         words = sb([P, E * C], U32, "slot_words")
         word_scales = sb([P, E * C], U8, "slot_scales")
@@ -112,68 +124,71 @@ def tile_moe_elr_gelu_kernel(tc, x_words, x_scales, w_words, w_scales, wa, wb_wo
         wa_scales = [sb([P, H], U8, "was%d" % e) for e in range(E)]
         h_codes = {}
         h_scales = {}
-        banks = {}
-
-        def wa_plane(e, first, count):
-            return wa_scales[e][:, first : first + count]
-
-        def quantize(e, first, count, values):
-            codes = wa_codes[e][:, first : first + count].bitcast(FP8X4)
-            nc.vector.quantize_mx(out=codes, scales=wa_plane(e, first, count), in_=values)
-
-        def cast_pair(e, u, copy, tag=None):
-            pair = sb([P, 2, P, PACK], BF16, "grouped%d_%d" % (e, u), tag)
-            source = wa_raw[e][:].rearrange("p j (m t) -> p m j t", t=PACK)[:, :, :, 2 * u : 2 * u + 2]
-            copy(pair[:].rearrange("p t m j -> p m j t"), source)
-            return pair[:]
-
-        def quantize_pair(e, u, pair):
-            quantize(e, 2 * u * P, 2 * P, pair.rearrange("p t m j -> p (t m j)"))
-
-        def cast_side(e, side, grouped):
-            source = wa_raw[e][:, :, side * H // 2 : (side + 1) * H // 2].rearrange("p j (m t) -> p m j t", t=PACK)
-            target = grouped[:, :, side * HALF_M : (side + 1) * HALF_M, :].rearrange("p t m j -> p m j t")
-            nc.scalar.copy(target, source)
-
-        def cast_rows(e, u, first, last, grouped, copy):
-            source = wa_raw[e][:].rearrange("p j (m t) -> p m j t", t=PACK)[:, first:last, :, 2 * u : 2 * u + 2]
-            copy(grouped[:, 2 * u : 2 * u + 2, first:last, :].rearrange("p t m j -> p m j t"), source)
 
         def own(e):
             return slice(e * C, (e + 1) * C)
 
-        def hidden(e, bank_tag, rounded, order):
+        def rounded_tile(e, tag=None):
+            return sb([P, PACK, P, PACK], BF16, "grouped%d" % e, tag)
+
+        def cast(e, grouped, ts, ms, copy):
+            source = wa_raw[e][:].rearrange("p j (m t) -> p m j t", t=PACK)[:, ms[0] : ms[1], :, ts[0] : ts[1]]
+            copy(grouped[:, ts[0] : ts[1], ms[0] : ms[1], :].rearrange("p t m j -> p m j t"), source)
+
+        def quantize(e, grouped, first, last):
+            codes = wa_codes[e][:, first * P : last * P].bitcast(FP8X4)
+            values = grouped[:, first:last, :, :].rearrange("p t m j -> p (t m j)")
+            nc.vector.quantize_mx(out=codes, scales=wa_scales[e][:, first * P : last * P], in_=values)
+
+        def cast_pair(e, u, copy):
+            pair = sb([P, 2, P, PACK], BF16, "pair%d_%d" % (e, u))
+            source = wa_raw[e][:].rearrange("p j (m t) -> p m j t", t=PACK)[:, :, :, 2 * u : 2 * u + 2]
+            copy(pair[:].rearrange("p t m j -> p m j t"), source)
+            return pair
+
+        def quantize_pair(e, u, pair):
+            cols = slice(2 * u * P, 2 * (u + 1) * P)
+            values = pair[:].rearrange("p t m j -> p (t m j)")
+            nc.vector.quantize_mx(out=wa_codes[e][:, cols].bitcast(FP8X4), scales=wa_scales[e][:, cols], in_=values)
+
+        def room(name, blocks, tag=None):
+            return sb([P, blocks * C], F32, name, tag)
+
+        def hidden(e, bank_tag, order, rounded=None):
             bank = psum.tile([P, PACK, C], F32, name="h_bank%d" % e, tag=bank_tag)
             for t in order:
                 cols = slice(t * P, (t + 1) * P)
                 nc.tensor.matmul_mx(
                     out=bank[:, t, :],
                     lhsT=wa_codes[e][:, cols].bitcast(FP8X4),
-                    lhsT_scale=wa_plane(e, t * P, P),
+                    lhsT_scale=wa_scales[e][:, cols],
                     rhs=words[:, own(e)].bitcast(FP8X4),
                     rhs_scale=word_scales[:, own(e)],
                     start=True,
                     stop=True,
                 )
+            if rounded is None:
+                rounded = room("h%d" % e, 2)[:].bitcast(BF16)
             nc.scalar.activation(rounded.rearrange("p (n t) -> p n t", t=PACK), bank[:].rearrange("p t n -> p n t"), GELU)
+            return rounded
 
-        def quantize_hidden(e, rounded, scales=None):
-            h_codes[e] = sb([P, C], U32, "h_codes%d" % e)
+        def quantize_hidden(e, rounded, scales=None, tag=None):
+            h_codes[e] = sb([P, C], U32, "h_codes%d" % e, tag)
             h_scales[e] = sb([P, C], U8, "h_scales%d" % e)[:] if scales is None else scales
             nc.vector.quantize_mx(out=h_codes[e][:].bitcast(FP8X4), scales=h_scales[e], in_=rounded)
 
-        def frozen(e, r, sums):
+        def frozen(e, r, sums, start=True):
             nc.tensor.matmul_mx(
                 out=sums,
                 lhsT=w_codes[e][:, 2 * r * P : 2 * (r + 1) * P].bitcast(FP4X4),
                 lhsT_scale=ws_plane[:, e, r * P : (r + 1) * P],
                 rhs=words[:, own(e)].bitcast(FP8X4),
                 rhs_scale=word_scales[:, own(e)],
-                start=True,
+                start=start,
                 stop=False,
             )
 
-        def adapter(e, r, sums):
+        def adapter(e, r, sums, stop=True):
             cols = slice(r * P, (r + 1) * P)
             nc.tensor.matmul_mx(
                 out=sums,
@@ -182,137 +197,138 @@ def tile_moe_elr_gelu_kernel(tc, x_words, x_scales, w_words, w_scales, wa, wb_wo
                 rhs=h_codes[e][:].bitcast(FP8X4),
                 rhs_scale=h_scales[e],
                 start=False,
-                stop=True,
+                stop=stop,
             )
 
-        def products(e, first, count, bank_tag):
-            bank = psum.tile([P, PACK * C], F32, name="y_bank%d_%d" % (e, first), tag=bank_tag)
-            for i in range(count):
-                frozen(e, first + i, bank[:, own(i)])
-                adapter(e, first + i, bank[:, own(i)])
-            banks[e, first] = bank[:, 0 : count * C]
+        def open_sums(e, rows, bank_tag):
+            bank = psum.tile([P, PACK, C], F32, name="y_bank%d_%d" % (e, rows[0]), tag=bank_tag)
+            for i, r in enumerate(rows):
+                frozen(e, r, bank[:, i, :], start=(i == 0))
+            return bank[:, 0 : len(rows), :]
 
-        def open_block(e, r, bank_tag):
-            bank = psum.tile([P, PACK * C], F32, name="y_bank%d_%d" % (e, r), tag=bank_tag)
-            banks[e, r] = bank[:, 0:C]
-            frozen(e, r, banks[e, r])
+        def close_sums(e, rows, sums):
+            for i, r in enumerate(rows):
+                adapter(e, r, sums[:, i, :], stop=(i == len(rows) - 1))
 
-        def scatter(r, first, last, values):
-            cols = offsets[:, first * LIST_COLS : last * LIST_COLS]
-            weights = gates[:, first * C : last * C]
-            nc.vector.tensor_tensor(windows[r][:].indirect(cols), values, weights, MULT)
+        def products(e, rows, bank_tag):
+            bank = psum.tile([P, PACK, C], F32, name="y_bank%d_%d" % (e, rows[0]), tag=bank_tag)
+            for i, r in enumerate(rows):
+                frozen(e, r, bank[:, i, :])
+                adapter(e, r, bank[:, i, :])
+            return bank[:, 0 : len(rows), :]
 
-        def room(name, blocks, tag=None):
-            return sb([P, blocks * C], F32, name, tag)
+        def blocks(flat):
+            return flat.rearrange("p (b c) -> p b c", c=C)
 
-        def send(e, first, count, staged):
-            nc.scalar.copy(staged, banks[e, first])
-            for i in range(count):
-                scatter(first + i, e, e + 1, staged[:, own(i)])
+        def weigh(e, target, sums):
+            weights = gates[:, own(e)].unsqueeze(1).to_broadcast(list(sums.shape))
+            nc.vector.tensor_tensor(target, sums, weights, MULT)
+
+        def slots(first, last):
+            return offsets[:, first * LIST_COLS : last * LIST_COLS]
+
+        def scatter_weighing(r, first, last, values):
+            nc.vector.tensor_tensor(windows[r][:].indirect(slots(first, last)), values, gates[:, first * C : last * C], MULT)
+
+        def scatter_vector(r, first, last, values):
+            nc.vector.tensor_copy(windows[r][:].indirect(slots(first, last)), values)
+
+        def scatter_scalar(r, first, last, values):
+            nc.scalar.activation(windows[r][:].indirect(slots(first, last)), values, COPY)
 
         def store(r):
             nc.sync.dma_start(out=out[r * P : (r + 1) * P, :], in_=windows[r][:])
 
-        def split_pair(e, u, tag=None):
-            pair = sb([P, 2, P, PACK], BF16, "grouped%d_%d" % (e, u), tag)
-            source = wa_raw[e][:].rearrange("p j (m t) -> p m j t", t=PACK)[:, :, :, 2 * u : 2 * u + 2]
-            target = pair[:].rearrange("p t m j -> p m j t")
-            nc.scalar.copy(target[:, 0:SCALAR_M, :, :], source[:, 0:SCALAR_M, :, :])
-            nc.vector.tensor_copy(target[:, SCALAR_M:P, :, :], source[:, SCALAR_M:P, :, :])
-            return pair[:]
+        def spread_gates(bank_tag):
+            spread = psum.tile([P, PACK, P], F32, name="gate_bank", tag=bank_tag)
+            for t in range(PACK):
+                nc.tensor.transpose(spread[:, t, :], gate_cols[:, t : t + 1].to_broadcast([P, P]), identity[:])
+            nc.scalar.copy(gates[:].rearrange("p (n t) -> p n t", t=PACK), spread[:].rearrange("p t n -> p n t"))
 
-        def shared_cast(e, tag):
-            late = cast_pair(e, 1, nc.vector.tensor_copy)
-            early = split_pair(e, 0) if e == 0 else cast_pair(e, 0, nc.scalar.copy, tag)
-            quantize_pair(e, 1, late)
-            for t in range(2):
-                quantize(e, t * P, P, early[:, t, :, :].rearrange("p m j -> p (m j)"))
+        vcopy = nc.vector.tensor_copy
+        scopy = nc.scalar.copy
 
-        def scalar_cast(e, tag):
-            return [cast_pair(e, 0, nc.scalar.copy, tag), split_pair(e, 1)]
+        grouped = rounded_tile(0)
+        cast(0, grouped, (2, 4), (0, P), vcopy)
+        cast(0, grouped, (0, 2), (0, SCALAR_M), scopy)
+        cast(0, grouped, (0, 2), (SCALAR_M, P), vcopy)
+        quantize(0, grouped, 2, 4)
+        quantize(0, grouped, 0, 1)
+        quantize(0, grouped, 1, 2)
+        spread_gates("bank7")
+        h0 = hidden(0, "bank0", (2, 3, 0, 1))
 
-        def activate(e, bank_tag, order):
-            rounded = room("h%d" % e, 2)[:].bitcast(BF16)
-            hidden(e, bank_tag, rounded, order)
-            quantize_hidden(e, rounded)
+        grouped = rounded_tile(1)
+        cast(1, grouped, (0, 4), (SCALAR_M, P), vcopy)
+        cast(1, grouped, (2, 4), (0, SCALAR_M), vcopy)
+        sums00 = open_sums(0, (0,), "bank1")
+        sums01 = open_sums(0, (1,), "bank2")
+        sums02 = open_sums(0, (2, 3), "bank3")
+        quantize_hidden(0, h0, ws_plane[:, 0, 0:C])
+        cast(1, grouped, (0, 2), (0, SCALAR_M), scopy)
+        quantize(1, grouped, 2, 4)
+        quantize(1, grouped, 0, 1)
+        quantize(1, grouped, 1, 2)
+        close_sums(0, (0,), sums00)
+        close_sums(0, (1,), sums01)
+        close_sums(0, (2, 3), sums02)
+        st00 = room("st00", 1)
+        st01 = room("st01", 1)
+        scopy(blocks(st01[:]), sums01)
+        weigh(0, blocks(st00[:]), sums00)
+        scatter_scalar(0, 0, 1, st00[:])
+        scatter_weighing(1, 0, 1, st01[:])
+        h1 = hidden(1, "bank2", (2, 3, 0, 1))
+        st02 = room("st02", 2, "wac1")
+        weigh(0, blocks(st02[:]), sums02)
+        scatter_scalar(2, 0, 1, st02[:, own(0)])
+        scatter_scalar(3, 0, 1, st02[:, own(1)])
 
-        shared_cast(0, None)
-        spread = psum.tile([P, PACK, P], F32, name="gate_bank", tag="bank7")
-        for t in range(PACK):
-            nc.tensor.transpose(spread[:, t, :], gate_cols[:, t : t + 1].to_broadcast([P, P]), identity[:])
-        nc.scalar.copy(gates[:].rearrange("p (n t) -> p n t", t=PACK), spread[:].rearrange("p t n -> p n t"))
-        rounded = room("h0", 2)[:].bitcast(BF16)
-        hidden(0, "bank0", rounded, (2, 3, 0, 1))
-        grouped = sb([P, PACK, P, PACK], BF16, "grouped1")
-        tail = wa_raw[1][:, :, PACK * SCALAR_M : H].rearrange("p j (m u t) -> p u m j t", u=2, t=2)
-        nc.vector.tensor_copy(grouped[:, :, SCALAR_M:P, :].rearrange("p (u t) m j -> p u m j t", u=2), tail)
-        cast_rows(1, 1, 0, SCALAR_M, grouped, nc.vector.tensor_copy)
-        for r, tag in enumerate(("bank1", "bank2", "bank4", "bank3")):
-            open_block(0, r, tag)
-        quantize_hidden(0, rounded, ws_plane[:, 0, 0:C])
-        cast_rows(1, 0, 0, SCALAR_M, grouped, nc.scalar.copy)
-        quantize_pair(1, 1, grouped[:, 2:4, :, :])
-        for t in range(2):
-            quantize(1, t * P, P, grouped[:, t, :, :].rearrange("p m j -> p (m j)"))
-        for r in range(R):
-            adapter(0, r, banks[0, r])
-        for r in range(2):
-            send(0, r, 1, room("st0%d" % r, 1)[:])
-        rounded = room("h1", 2)[:].bitcast(BF16)
-        hidden(1, "bank1", rounded, (2, 3, 0, 1))
-        staged = room("st02", 2, "wac1")
-        for i in range(2):
-            send(0, 2 + i, 1, staged[:, own(i)])
-        for r, tag in enumerate(("bank5", "bank6", "bank0", "bank7")):
-            open_block(1, r, tag)
-        quantize_hidden(1, rounded)
-        for r in range(R):
-            adapter(1, r, banks[1, r])
+        late = cast_pair(2, 1, vcopy)
+        early = cast_pair(2, 0, vcopy)
+        quantize_pair(2, 1, late)
+        quantize_hidden(1, h1, tag="pair2_1")
+        quantize_pair(2, 0, early)
+        h2 = hidden(2, "bank5", (2, 3, 0, 1))
+        sums10 = open_sums(1, (0, 1), "bank0")
+        sums12 = open_sums(1, (2, 3), "bank1")
+        close_sums(1, (0, 1), sums10)
+        close_sums(1, (2, 3), sums12)
+        st10 = room("st10", 2)
+        weigh(1, blocks(st10[:]), sums10)
+        scatter_scalar(0, 1, 2, st10[:, own(0)])
+        scatter_scalar(1, 1, 2, st10[:, own(1)])
 
-        def spent(e, row, side):
-            return wa_raw[e][:, row, side * H // 2 : side * H // 2 + C]
-
-        def finish(e, grouped, last):
-            cast_rows(e, 0, HALF_M, P, grouped, nc.scalar.copy)
-            cast_rows(e, 1, HALF_M, last, grouped, nc.scalar.copy)
-            if last < P:
-                cast_rows(e, 1, last, P, grouped, nc.vector.tensor_copy)
-            quantize_pair(e, 0, grouped[:, 0:2, :, :])
-            for t in (2, 3):
-                quantize(e, t * P, P, grouped[:, t, :, :].rearrange("p m j -> p (m j)"))
-
-        grouped = sb([P, PACK, P, PACK], BF16, "grouped2", "was1")
-        cast_side(2, 0, grouped)
-        send(1, 0, 1, spent(2, 0, 0))
-        finish(2, grouped, P)
-        for r in (1, 2):
-            send(1, r, 1, spent(2, r, 1))
-        grouped = sb([P, PACK, P, PACK], BF16, "grouped3")
-        cast_side(3, 0, grouped)
-        rounded = wa_raw[3][:, 0, 0 : H // 2].bitcast(BF16)
-        hidden(2, "bank5", rounded, (0, 1, 2, 3))
-        open_block(2, 0, "bank2")
-        quantize_hidden(2, rounded)
-        adapter(2, 0, banks[2, 0])
-        finish(3, grouped, P)
-        send(1, 3, 1, spent(3, 1, 1))
-        send(2, 0, 1, spent(3, 0, 1))
-        rounded = room("h3", 2)[:].bitcast(BF16)
-        hidden(3, "bank1", rounded, (0, 1, 2, 3))
-        last = room("st21", 4, "wac3")
-        products(2, 1, 1, "bank2")
-        products(2, 2, 2, "bank7")
-        send(2, 1, 1, last[:, 0:C])
-        nc.scalar.copy(last[:, C : 3 * C], banks[2, 2])
-        scatter(2, 2, 3, last[:, C : 2 * C])
-        for r, tag in enumerate(("bank5", "bank6", "bank0", "bank3")):
-            open_block(3, r, tag)
-        quantize_hidden(3, rounded)
-        for r in range(R):
-            adapter(3, r, banks[3, r])
-        for r in range(R - 1):
-            send(3, r, 1, room("st3%d" % r, 1)[:])
-            store(r)
-        nc.scalar.copy(last[:, 3 * C :], banks[3, 3])
-        scatter(3, 2, 4, last[:, 2 * C :])
+        late = cast_pair(3, 1, vcopy)
+        early = cast_pair(3, 0, vcopy)
+        quantize_pair(3, 1, late)
+        quantize_hidden(2, h2, tag="pair3_1")
+        quantize_pair(3, 0, early)
+        h3 = hidden(3, "bank6", (2, 3, 0, 1))
+        st12 = room("st12", 2, "pair3_0")
+        weigh(1, blocks(st12[:]), sums12)
+        sums20 = products(2, (0,), "bank4")
+        st20 = room("st20", 1)
+        weigh(2, blocks(st20[:]), sums20)
+        scatter_vector(2, 1, 2, st12[:, own(0)])
+        scatter_scalar(0, 2, 3, st20[:])
+        sums30 = open_sums(3, (0,), "bank2")
+        sums31 = open_sums(3, (1, 2, 3), "bank7")
+        sums21 = products(2, (1, 2, 3), "bank3")
+        quantize_hidden(3, h3)
+        close_sums(3, (0,), sums30)
+        close_sums(3, (1, 2, 3), sums31)
+        rest = sb([P, 3, 2, C], F32, "rest", "h3")
+        st30 = room("st30", 1)
+        weigh(2, rest[:, :, 0, :], sums21)
+        weigh(3, blocks(st30[:]), sums30)
+        scatter_scalar(0, 3, 4, st30[:])
+        store(0)
+        weigh(3, rest[:, :, 1, :], sums31)
+        scatter_vector(1, 2, 4, rest[:, 0, :, :].rearrange("p e c -> p (e c)"))
+        store(1)
+        scatter_scalar(2, 2, 4, rest[:, 1, :, :].rearrange("p e c -> p (e c)"))
+        scatter_scalar(3, 1, 2, st12[:, own(1)])
+        store(2)
+        scatter_vector(3, 2, 4, rest[:, 2, :, :].rearrange("p e c -> p (e c)"))
         store(3)

@@ -100,7 +100,7 @@ def tile_moe_elr_gelu_kernel(tc, x_words, x_scales, w_words, w_scales, wa, wb_wo
             load_xs(q)
         load_wa(0)
         load_gate()
-        load_ws(0, 2)
+        load_ws(0, 4)
         load_wa(1)
         load_w(0, 1)
         load_wb(0, 1)
@@ -110,9 +110,9 @@ def tile_moe_elr_gelu_kernel(tc, x_words, x_scales, w_words, w_scales, wa, wb_wo
         load_w(1, 2)
         load_wb(1, 2)
         load_wa(3)
-        load_ws(2, 4)
-        load_w(2, 4)
+        load_w(2, 3)
         load_wb(2, 3)
+        load_w(3, 4)
         load_wb(3, 4)
 
         words = sb([P, E * C], U32, "slot_words")
@@ -286,49 +286,45 @@ def tile_moe_elr_gelu_kernel(tc, x_words, x_scales, w_words, w_scales, wa, wb_wo
 
         late = cast_pair(2, 1, vcopy)
         early = cast_pair(2, 0, vcopy)
-        quantize_pair(2, 1, late)
-        quantize_hidden(1, h1, tag="pair2_1")
-        quantize_pair(2, 0, early)
-        h2 = hidden(2, "bank5", (2, 3, 0, 1))
         sums10 = open_sums(1, (0, 1), "bank0")
         sums12 = open_sums(1, (2, 3), "bank1")
+        quantize_hidden(1, h1, ws_plane[:, 1, 0:C])
+        quantize_pair(2, 1, late)
+        quantize_pair(2, 0, early)
         close_sums(1, (0, 1), sums10)
         close_sums(1, (2, 3), sums12)
-        st10 = room("st10", 2)
-        weigh(1, blocks(st10[:]), sums10)
-        scatter_scalar(0, 1, 2, st10[:, own(0)])
-        scatter_scalar(1, 1, 2, st10[:, own(1)])
+        staged = sb([P, R, E - 1, C], F32, "staged")
+        weigh(1, staged[:, 0:2, 0, :], sums10)
+        weigh(1, staged[:, 2:4, 0, :], sums12)
+        scatter_scalar(0, 1, 2, staged[:, 0, 0, :])
+        scatter_scalar(1, 1, 2, staged[:, 1, 0, :])
+        h2 = hidden(2, "bank0", (2, 3, 0, 1))
 
         late = cast_pair(3, 1, vcopy)
         early = cast_pair(3, 0, vcopy)
         quantize_pair(3, 1, late)
-        quantize_hidden(2, h2, tag="pair3_1")
         quantize_pair(3, 0, early)
         h3 = hidden(3, "bank6", (2, 3, 0, 1))
-        st12 = room("st12", 2, "pair3_0")
-        weigh(1, blocks(st12[:]), sums12)
-        sums20 = products(2, (0,), "bank4")
-        st20 = room("st20", 1)
-        weigh(2, blocks(st20[:]), sums20)
-        scatter_vector(2, 1, 2, st12[:, own(0)])
-        scatter_scalar(0, 2, 3, st20[:])
+        sums20 = open_sums(2, (0,), "bank4")
         sums30 = open_sums(3, (0,), "bank2")
+        sums21 = open_sums(2, (1, 2, 3), "bank3")
         sums31 = open_sums(3, (1, 2, 3), "bank7")
-        sums21 = products(2, (1, 2, 3), "bank3")
+        quantize_hidden(2, h2, tag="pair3_0")
+        close_sums(2, (0,), sums20)
+        weigh(2, staged[:, 0:1, 1, :], sums20)
+        scatter_scalar(0, 2, 3, staged[:, 0, 1, :])
         quantize_hidden(3, h3)
         close_sums(3, (0,), sums30)
+        close_sums(2, (1, 2, 3), sums21)
         close_sums(3, (1, 2, 3), sums31)
-        rest = sb([P, 3, 2, C], F32, "rest", "h3")
-        st30 = room("st30", 1)
-        weigh(2, rest[:, :, 0, :], sums21)
-        weigh(3, blocks(st30[:]), sums30)
-        scatter_scalar(0, 3, 4, st30[:])
+        weigh(3, staged[:, 0:1, 2, :], sums30)
+        scatter_scalar(0, 3, 4, staged[:, 0, 2, :])
         store(0)
-        weigh(3, rest[:, :, 1, :], sums31)
-        scatter_vector(1, 2, 4, rest[:, 0, :, :].rearrange("p e c -> p (e c)"))
+        weigh(2, staged[:, 1:4, 1, :], sums21)
+        weigh(3, staged[:, 1:4, 2, :], sums31)
+        scatter_vector(1, 2, 4, staged[:, 1, 1:3, :].rearrange("p e c -> p (e c)"))
         store(1)
-        scatter_scalar(2, 2, 4, rest[:, 1, :, :].rearrange("p e c -> p (e c)"))
-        scatter_scalar(3, 1, 2, st12[:, own(1)])
+        scatter_scalar(2, 1, 4, staged[:, 2, :, :].rearrange("p e c -> p (e c)"))
         store(2)
-        scatter_vector(3, 2, 4, rest[:, 2, :, :].rearrange("p e c -> p (e c)"))
+        scatter_vector(3, 1, 4, staged[:, 3, :, :].rearrange("p e c -> p (e c)"))
         store(3)

@@ -39,7 +39,8 @@ def tile_moe_elr_gelu_kernel(tc, x_words, x_scales, w_words, w_scales, wa, wb_wo
         offsets = keep.tile([P, E * LIST_COLS], U16, name="offsets")
         x_table = sb([P, T], I32, "x_table")
         xs_table = sb([P, T], U8, "xs_table")
-        ws_plane = sb([P, E, N], U8, "ws_plane")
+        ws_halves = [sb([P, 2, N], U8, "ws_plane%d" % i) for i in range(2)]
+        ws_plane = [ws_halves[e // 2][:, e % 2, :] for e in range(E)]
         wbs_plane = sb([P, N], U8, "wbs_plane")
         gate_cols = sb([P, PACK], F32, "gate_cols")
         gates = sb([P, E * C], F32, "gates")
@@ -52,8 +53,9 @@ def tile_moe_elr_gelu_kernel(tc, x_words, x_scales, w_words, w_scales, wa, wb_wo
 
         nc.vector.memset(xs_table[:].bitcast(I32), 0)
         nc.vector.memset(windows[0][:], 0.0)
-        nc.vector.memset(ws_plane[:].rearrange("p e n -> p (e n)").bitcast(I32), 0)
+        nc.vector.memset(ws_halves[0][:].rearrange("p e n -> p (e n)").bitcast(I32), 0)
         nc.vector.memset(wbs_plane[:].bitcast(I32), 0)
+        nc.vector.memset(ws_halves[1][:].rearrange("p e n -> p (e n)").bitcast(I32), 0)
         nc.vector.tensor_copy(windows[1][:], windows[0][:])
         for r in (2, 3):
             nc.scalar.activation(windows[r][:], windows[0][:], GELU)
@@ -82,7 +84,7 @@ def tile_moe_elr_gelu_kernel(tc, x_words, x_scales, w_words, w_scales, wa, wb_wo
         def load_ws(first, last):
             for q in range(QUADS):
                 rows = w_scales[first:last, 0, q:16:4, :].bitcast(I32).rearrange("e b n -> b e n")
-                nc.sync.dma_start(out=ws_plane[q:P:32, first:last, :].bitcast(I32), in_=rows)
+                nc.sync.dma_start(out=ws_halves[first // 2][q:P:32, first % 2 : first % 2 + last - first, :].bitcast(I32), in_=rows)
 
         def load_wbs(q):
             rows = wb_scales[:, 0, 4 * q : 4 * q + 4, :].bitcast(I32)
@@ -100,7 +102,7 @@ def tile_moe_elr_gelu_kernel(tc, x_words, x_scales, w_words, w_scales, wa, wb_wo
             load_xs(q)
         load_wa(0)
         load_gate()
-        load_ws(0, 4)
+        load_ws(0, 2)
         load_wa(1)
         load_w(0, 1)
         load_wb(0, 1)
@@ -110,9 +112,9 @@ def tile_moe_elr_gelu_kernel(tc, x_words, x_scales, w_words, w_scales, wa, wb_wo
         load_w(1, 2)
         load_wb(1, 2)
         load_wa(3)
-        load_w(2, 3)
         load_wb(2, 3)
-        load_w(3, 4)
+        load_ws(2, 4)
+        load_w(2, 4)
         load_wb(3, 4)
 
         words = sb([P, E * C], U32, "slot_words")
@@ -122,6 +124,7 @@ def tile_moe_elr_gelu_kernel(tc, x_words, x_scales, w_words, w_scales, wa, wb_wo
 
         wa_codes = [sb([P, H], U32, "wac%d" % e) for e in range(E)]
         wa_scales = [sb([P, H], U8, "was%d" % e) for e in range(E)]
+        wa_planes = {(e, u): wa_scales[e][:, 2 * u * P : 2 * (u + 1) * P] for e in range(E) for u in range(2)}
         h_codes = {}
         h_scales = {}
 
@@ -140,16 +143,18 @@ def tile_moe_elr_gelu_kernel(tc, x_words, x_scales, w_words, w_scales, wa, wb_wo
             values = grouped[:, first:last, :, :].rearrange("p t m j -> p (t m j)")
             nc.vector.quantize_mx(out=codes, scales=wa_scales[e][:, first * P : last * P], in_=values)
 
-        def cast_pair(e, u, copy):
-            pair = sb([P, 2, P, PACK], BF16, "pair%d_%d" % (e, u))
+        def cast_pair(e, u, copy, tag=None):
+            pair = sb([P, 2, P, PACK], BF16, "pair%d_%d" % (e, u), tag)
             source = wa_raw[e][:].rearrange("p j (m t) -> p m j t", t=PACK)[:, :, :, 2 * u : 2 * u + 2]
             copy(pair[:].rearrange("p t m j -> p m j t"), source)
             return pair
 
-        def quantize_pair(e, u, pair):
+        def quantize_pair(e, u, pair, plane=None):
             cols = slice(2 * u * P, 2 * (u + 1) * P)
             values = pair[:].rearrange("p t m j -> p (t m j)")
-            nc.vector.quantize_mx(out=wa_codes[e][:, cols].bitcast(FP8X4), scales=wa_scales[e][:, cols], in_=values)
+            if plane is not None:
+                wa_planes[e, u] = plane
+            nc.vector.quantize_mx(out=wa_codes[e][:, cols].bitcast(FP8X4), scales=wa_planes[e, u], in_=values)
 
         def room(name, blocks, tag=None):
             return sb([P, blocks * C], F32, name, tag)
@@ -161,7 +166,7 @@ def tile_moe_elr_gelu_kernel(tc, x_words, x_scales, w_words, w_scales, wa, wb_wo
                 nc.tensor.matmul_mx(
                     out=bank[:, t, :],
                     lhsT=wa_codes[e][:, cols].bitcast(FP8X4),
-                    lhsT_scale=wa_scales[e][:, cols],
+                    lhsT_scale=wa_planes[e, t // 2][:, (t % 2) * P : (t % 2 + 1) * P],
                     rhs=words[:, own(e)].bitcast(FP8X4),
                     rhs_scale=word_scales[:, own(e)],
                     start=True,
@@ -181,7 +186,7 @@ def tile_moe_elr_gelu_kernel(tc, x_words, x_scales, w_words, w_scales, wa, wb_wo
             nc.tensor.matmul_mx(
                 out=sums,
                 lhsT=w_codes[e][:, 2 * r * P : 2 * (r + 1) * P].bitcast(FP4X4),
-                lhsT_scale=ws_plane[:, e, r * P : (r + 1) * P],
+                lhsT_scale=ws_plane[e][:, r * P : (r + 1) * P],
                 rhs=words[:, own(e)].bitcast(FP8X4),
                 rhs_scale=word_scales[:, own(e)],
                 start=start,
@@ -264,7 +269,7 @@ def tile_moe_elr_gelu_kernel(tc, x_words, x_scales, w_words, w_scales, wa, wb_wo
         sums00 = open_sums(0, (0,), "bank1")
         sums01 = open_sums(0, (1,), "bank2")
         sums02 = open_sums(0, (2, 3), "bank3")
-        quantize_hidden(0, h0, ws_plane[:, 0, 0:C])
+        quantize_hidden(0, h0, ws_plane[0][:, 0:C])
         cast(1, grouped, (0, 2), (0, SCALAR_M), scopy)
         quantize(1, grouped, 2, 4)
         quantize(1, grouped, 0, 1)
@@ -285,46 +290,57 @@ def tile_moe_elr_gelu_kernel(tc, x_words, x_scales, w_words, w_scales, wa, wb_wo
         scatter_scalar(3, 0, 1, st02[:, own(1)])
 
         late = cast_pair(2, 1, vcopy)
-        early = cast_pair(2, 0, vcopy)
         sums10 = open_sums(1, (0, 1), "bank0")
         sums12 = open_sums(1, (2, 3), "bank1")
-        quantize_hidden(1, h1, ws_plane[:, 1, 0:C])
-        quantize_pair(2, 1, late)
-        quantize_pair(2, 0, early)
+        quantize_hidden(1, h1, ws_plane[1][:, 0:C])
+        quantize_pair(2, 1, late, ws_plane[1][:, C : 3 * C])
+        early = cast_pair(2, 0, vcopy, "h1")
         close_sums(1, (0, 1), sums10)
         close_sums(1, (2, 3), sums12)
-        staged = sb([P, R, E - 1, C], F32, "staged")
-        weigh(1, staged[:, 0:2, 0, :], sums10)
-        weigh(1, staged[:, 2:4, 0, :], sums12)
-        scatter_scalar(0, 1, 2, staged[:, 0, 0, :])
-        scatter_scalar(1, 1, 2, staged[:, 1, 0, :])
+        st10 = room("st10", 2)
+        weigh(1, blocks(st10[:]), sums10)
+        quantize_pair(2, 0, early)
+        scatter_scalar(0, 1, 2, st10[:, own(0)])
+        scatter_scalar(1, 1, 2, st10[:, own(1)])
         h2 = hidden(2, "bank0", (2, 3, 0, 1))
 
         late = cast_pair(3, 1, vcopy)
         early = cast_pair(3, 0, vcopy)
+        st12 = room("st12", 2, "raw3")
         quantize_pair(3, 1, late)
+        weigh(1, blocks(st12[:, own(1)]), sums12[:, 1:2, :])
         quantize_pair(3, 0, early)
+        scatter_scalar(3, 1, 2, st12[:, own(1)])
         h3 = hidden(3, "bank6", (2, 3, 0, 1))
-        sums20 = open_sums(2, (0,), "bank4")
+        vcopy(blocks(st12[:, own(0)]), sums12[:, 0:1, :])
+        quantize_hidden(2, h2, tag="pair3_1")
+        scatter_weighing(2, 1, 2, st12[:, own(0)])
+        sums20 = products(2, (0,), "bank4")
+        sums22 = products(2, (2,), "bank5")
+        sums21 = products(2, (1, 3), "bank3")
         sums30 = open_sums(3, (0,), "bank2")
-        sums21 = open_sums(2, (1, 2, 3), "bank3")
-        sums31 = open_sums(3, (1, 2, 3), "bank7")
-        quantize_hidden(2, h2, tag="pair3_0")
-        close_sums(2, (0,), sums20)
-        weigh(2, staged[:, 0:1, 1, :], sums20)
-        scatter_scalar(0, 2, 3, staged[:, 0, 1, :])
-        quantize_hidden(3, h3)
+        sums31 = open_sums(3, (1, 3), "bank7")
+        sums32 = open_sums(3, (2,), "bank0")
+        st20 = room("st20", 1)
+        st22 = sb([P, 2, C], F32, "st22")
+        weigh(2, blocks(st20[:]), sums20)
+        scatter_scalar(0, 2, 3, st20[:])
+        weigh(2, st22[:, 0:1, :], sums22)
+        quantize_hidden(3, h3, ws_plane[2][:, C : 2 * C])
         close_sums(3, (0,), sums30)
-        close_sums(2, (1, 2, 3), sums21)
-        close_sums(3, (1, 2, 3), sums31)
-        weigh(3, staged[:, 0:1, 2, :], sums30)
-        scatter_scalar(0, 3, 4, staged[:, 0, 2, :])
+        close_sums(3, (1, 3), sums31)
+        close_sums(3, (2,), sums32)
+        rest = sb([P, 2, 2, C], F32, "rest", "h3")
+        scopy(rest[:, :, 0, :], sums21)
+        st30 = room("st30", 1)
+        weigh(3, blocks(st30[:]), sums30)
+        scatter_scalar(0, 3, 4, st30[:])
         store(0)
-        weigh(2, staged[:, 1:4, 1, :], sums21)
-        weigh(3, staged[:, 1:4, 2, :], sums31)
-        scatter_vector(1, 2, 4, staged[:, 1, 1:3, :].rearrange("p e c -> p (e c)"))
+        vcopy(rest[:, :, 1, :], sums31)
+        weigh(3, st22[:, 1:2, :], sums32)
+        scatter_weighing(1, 2, 4, rest[:, 0, :, :].rearrange("p e c -> p (e c)"))
         store(1)
-        scatter_scalar(2, 1, 4, staged[:, 2, :, :].rearrange("p e c -> p (e c)"))
+        scatter_scalar(2, 2, 4, st22[:].rearrange("p e c -> p (e c)"))
         store(2)
-        scatter_vector(3, 1, 4, staged[:, 3, :, :].rearrange("p e c -> p (e c)"))
+        scatter_weighing(3, 2, 4, rest[:, 1, :, :].rearrange("p e c -> p (e c)"))
         store(3)

@@ -110,8 +110,8 @@ def tile_moe_elr_gelu_kernel(tc, x_words, x_scales, w_words, w_scales, wa, wb_wo
             load_wbs(q)
         load_wa(2)
         load_w(1, 2)
-        load_wb(1, 2)
         load_wa(3)
+        load_wb(1, 2)
         load_wb(2, 3)
         load_ws(2, 4)
         load_w(2, 4)
@@ -290,57 +290,61 @@ def tile_moe_elr_gelu_kernel(tc, x_words, x_scales, w_words, w_scales, wa, wb_wo
         scatter_scalar(3, 0, 1, st02[:, own(1)])
 
         late = cast_pair(2, 1, vcopy)
-        sums10 = open_sums(1, (0, 1), "bank0")
-        sums12 = open_sums(1, (2, 3), "bank1")
+        early = cast_pair(2, 0, vcopy)
+        sums10 = open_sums(1, (0,), "bank0")
+        sums11 = open_sums(1, (1,), "bank1")
+        sums12 = open_sums(1, (2, 3), "bank4")
         quantize_hidden(1, h1, ws_plane[1][:, 0:C])
-        quantize_pair(2, 1, late, ws_plane[1][:, C : 3 * C])
-        early = cast_pair(2, 0, vcopy, "h1")
-        close_sums(1, (0, 1), sums10)
-        close_sums(1, (2, 3), sums12)
-        st10 = room("st10", 2)
-        weigh(1, blocks(st10[:]), sums10)
+        quantize_pair(2, 1, late)
         quantize_pair(2, 0, early)
-        scatter_scalar(0, 1, 2, st10[:, own(0)])
-        scatter_scalar(1, 1, 2, st10[:, own(1)])
-        h2 = hidden(2, "bank0", (2, 3, 0, 1))
 
-        late = cast_pair(3, 1, vcopy)
-        early = cast_pair(3, 0, vcopy)
-        st12 = room("st12", 2, "raw3")
-        quantize_pair(3, 1, late)
-        weigh(1, blocks(st12[:, own(1)]), sums12[:, 1:2, :])
-        quantize_pair(3, 0, early)
-        scatter_scalar(3, 1, 2, st12[:, own(1)])
+        grouped = rounded_tile(3)
+        cast(3, grouped, (2, 4), (0, P), vcopy)
+        cast(3, grouped, (0, 2), (0, SCALAR_M), scopy)
+        cast(3, grouped, (0, 2), (SCALAR_M, P), vcopy)
+        h2 = hidden(2, "bank5", (2, 3, 0, 1), wa_raw[3][:, 0, 0 : H // 2].bitcast(BF16))
+        close_sums(1, (0,), sums10)
+        close_sums(1, (1,), sums11)
+        close_sums(1, (2, 3), sums12)
+        quantize(3, grouped, 2, 4)
+        st10 = room("st10", 1)
+        weigh(1, blocks(st10[:]), sums10)
+        scatter_scalar(0, 1, 2, st10[:])
+        quantize(3, grouped, 0, 1)
+        quantize(3, grouped, 1, 2)
         h3 = hidden(3, "bank6", (2, 3, 0, 1))
-        vcopy(blocks(st12[:, own(0)]), sums12[:, 0:1, :])
-        quantize_hidden(2, h2, tag="pair3_1")
-        scatter_weighing(2, 1, 2, st12[:, own(0)])
-        sums20 = products(2, (0,), "bank4")
-        sums22 = products(2, (2,), "bank5")
+        st11 = room("st11", 1, "grouped3")
+        vcopy(blocks(st11[:]), sums11)
+        quantize_hidden(2, h2)
+        plain = sb([P, 2, E - 1, C], F32, "plain", "wac3")
+        weighted = sb([P, E - 1, C], F32, "weighted")
+        weigh(1, weighted[:, 0:1, :], sums12[:, 0:1, :])
+        scatter_weighing(1, 1, 2, st11[:])
+        scopy(plain[:, 1, 0:1, :], sums12[:, 1:2, :])
+        sums20 = products(2, (0,), "bank2")
+        sums30 = open_sums(3, (0,), "bank0")
         sums21 = products(2, (1, 3), "bank3")
-        sums30 = open_sums(3, (0,), "bank2")
+        sums22 = products(2, (2,), "bank5")
         sums31 = open_sums(3, (1, 3), "bank7")
-        sums32 = open_sums(3, (2,), "bank0")
+        sums32 = open_sums(3, (2,), "bank1")
+        quantize_hidden(3, h3, ws_plane[2][:, C : 2 * C])
         st20 = room("st20", 1)
-        st22 = sb([P, 2, C], F32, "st22")
         weigh(2, blocks(st20[:]), sums20)
         scatter_scalar(0, 2, 3, st20[:])
-        weigh(2, st22[:, 0:1, :], sums22)
-        quantize_hidden(3, h3, ws_plane[2][:, C : 2 * C])
         close_sums(3, (0,), sums30)
         close_sums(3, (1, 3), sums31)
         close_sums(3, (2,), sums32)
-        rest = sb([P, 2, 2, C], F32, "rest", "h3")
-        scopy(rest[:, :, 0, :], sums21)
+        vcopy(plain[:, :, 1, :], sums21)
         st30 = room("st30", 1)
         weigh(3, blocks(st30[:]), sums30)
         scatter_scalar(0, 3, 4, st30[:])
         store(0)
-        vcopy(rest[:, :, 1, :], sums31)
-        weigh(3, st22[:, 1:2, :], sums32)
-        scatter_weighing(1, 2, 4, rest[:, 0, :, :].rearrange("p e c -> p (e c)"))
+        vcopy(plain[:, :, 2, :], sums31)
+        weigh(2, weighted[:, 1:2, :], sums22)
+        weigh(3, weighted[:, 2:3, :], sums32)
+        scatter_weighing(1, 2, 4, plain[:, 0, 1:3, :].rearrange("p e c -> p (e c)"))
         store(1)
-        scatter_scalar(2, 2, 4, st22[:].rearrange("p e c -> p (e c)"))
+        scatter_scalar(2, 1, 4, weighted[:].rearrange("p e c -> p (e c)"))
         store(2)
-        scatter_weighing(3, 2, 4, rest[:, 1, :, :].rearrange("p e c -> p (e c)"))
+        scatter_weighing(3, 1, 4, plain[:, 1, :, :].rearrange("p e c -> p (e c)"))
         store(3)

@@ -25,6 +25,7 @@ R = N // P
 LIST_COLS = C // 16
 ALIGN = 64
 SCALAR_M = 96
+HALF_M = P // 2
 
 
 def tile_moe_elr_gelu_kernel(tc, x_words, x_scales, w_words, w_scales, wa, wb_words, wb_scales, gate, offs, out):
@@ -292,56 +293,57 @@ def tile_moe_elr_gelu_kernel(tc, x_words, x_scales, w_words, w_scales, wa, wb_wo
         late = cast_pair(2, 1, vcopy)
         early = cast_pair(2, 0, vcopy)
         sums10 = open_sums(1, (0,), "bank0")
-        sums11 = open_sums(1, (1,), "bank1")
-        sums12 = open_sums(1, (2, 3), "bank4")
-        quantize_hidden(1, h1, ws_plane[1][:, 0:C])
+        sums11 = open_sums(1, (1, 3), "bank1")
+        sums12 = open_sums(1, (2,), "bank4")
         quantize_pair(2, 1, late)
         quantize_pair(2, 0, early)
+        quantize_hidden(1, h1, tag="pair2_1")
 
         grouped = rounded_tile(3)
-        cast(3, grouped, (2, 4), (0, P), vcopy)
-        cast(3, grouped, (0, 2), (0, SCALAR_M), scopy)
-        cast(3, grouped, (0, 2), (SCALAR_M, P), vcopy)
+        cast(3, grouped, (0, 4), (0, HALF_M), vcopy)
+        cast(3, grouped, (0, 2), (HALF_M, P), scopy)
+        cast(3, grouped, (2, 4), (HALF_M, P), vcopy)
         h2 = hidden(2, "bank5", (2, 3, 0, 1), wa_raw[3][:, 0, 0 : H // 2].bitcast(BF16))
         close_sums(1, (0,), sums10)
-        close_sums(1, (1,), sums11)
-        close_sums(1, (2, 3), sums12)
-        quantize(3, grouped, 2, 4)
+        close_sums(1, (1, 3), sums11)
+        close_sums(1, (2,), sums12)
+        quantize(3, grouped, 0, 2)
         st10 = room("st10", 1)
         weigh(1, blocks(st10[:]), sums10)
+        st11 = room("st11", 1)
+        weighted = sb([P, E - 1, C], F32, "weighted")
+        scopy(blocks(st11[:]), sums11[:, 0:1, :])
         scatter_scalar(0, 1, 2, st10[:])
-        quantize(3, grouped, 0, 1)
-        quantize(3, grouped, 1, 2)
-        h3 = hidden(3, "bank6", (2, 3, 0, 1))
-        st11 = room("st11", 1, "grouped3")
-        vcopy(blocks(st11[:]), sums11)
+        quantize(3, grouped, 2, 3)
+        quantize(3, grouped, 3, 4)
+        h3 = hidden(3, "bank6", (0, 1, 2, 3))
         quantize_hidden(2, h2)
         plain = sb([P, 2, E - 1, C], F32, "plain", "wac3")
-        weighted = sb([P, E - 1, C], F32, "weighted")
-        weigh(1, weighted[:, 0:1, :], sums12[:, 0:1, :])
+        scopy(plain[:, 1:2, 0, :], sums11[:, 1:2, :])
         scatter_weighing(1, 1, 2, st11[:])
-        scopy(plain[:, 1, 0:1, :], sums12[:, 1:2, :])
         sums20 = products(2, (0,), "bank2")
         sums30 = open_sums(3, (0,), "bank0")
         sums21 = products(2, (1, 3), "bank3")
-        sums22 = products(2, (2,), "bank5")
+        pair22 = psum.tile([P, PACK, C], F32, name="y_bank22", tag="bank5")
+        frozen(2, 2, pair22[:, 0, :])
+        adapter(2, 2, pair22[:, 0, :])
         sums31 = open_sums(3, (1, 3), "bank7")
-        sums32 = open_sums(3, (2,), "bank1")
-        quantize_hidden(3, h3, ws_plane[2][:, C : 2 * C])
+        frozen(3, 2, pair22[:, 1, :])
         st20 = room("st20", 1)
         weigh(2, blocks(st20[:]), sums20)
         scatter_scalar(0, 2, 3, st20[:])
+        weigh(1, weighted[:, 0:1, :], sums12)
+        quantize_hidden(3, h3, ws_plane[2][:, C : 2 * C])
         close_sums(3, (0,), sums30)
         close_sums(3, (1, 3), sums31)
-        close_sums(3, (2,), sums32)
+        adapter(3, 2, pair22[:, 1, :])
         vcopy(plain[:, :, 1, :], sums21)
         st30 = room("st30", 1)
         weigh(3, blocks(st30[:]), sums30)
         scatter_scalar(0, 3, 4, st30[:])
         store(0)
         vcopy(plain[:, :, 2, :], sums31)
-        weigh(2, weighted[:, 1:2, :], sums22)
-        weigh(3, weighted[:, 2:3, :], sums32)
+        nc.vector.tensor_tensor(weighted[:, 1:3, :], pair22[:, 0:2, :], blocks(gates[:, 2 * C : 4 * C]), MULT)
         scatter_weighing(1, 2, 4, plain[:, 0, 1:3, :].rearrange("p e c -> p (e c)"))
         store(1)
         scatter_scalar(2, 1, 4, weighted[:].rearrange("p e c -> p (e c)"))

@@ -115,7 +115,8 @@ def tile_moe_elr_gelu_kernel(tc, x_words, x_scales, w_words, w_scales, wa, wb_wo
         load_wb(1, 2)
         load_wb(2, 3)
         load_ws(2, 4)
-        load_w(2, 4)
+        load_w(2, 3)
+        load_w(3, 4)
         load_wb(3, 4)
 
         words = sb([P, E * C], U32, "slot_words")
@@ -269,7 +270,8 @@ def tile_moe_elr_gelu_kernel(tc, x_words, x_scales, w_words, w_scales, wa, wb_wo
         cast(1, grouped, (2, 4), (0, SCALAR_M), vcopy)
         sums00 = open_sums(0, (0,), "bank1")
         sums01 = open_sums(0, (1,), "bank2")
-        sums02 = open_sums(0, (2, 3), "bank3")
+        sums02 = open_sums(0, (2,), "bank3")
+        sums03 = open_sums(0, (3,), "bank4")
         quantize_hidden(0, h0, ws_plane[0][:, 0:C])
         cast(1, grouped, (0, 2), (0, SCALAR_M), scopy)
         quantize(1, grouped, 2, 4)
@@ -277,23 +279,26 @@ def tile_moe_elr_gelu_kernel(tc, x_words, x_scales, w_words, w_scales, wa, wb_wo
         quantize(1, grouped, 1, 2)
         close_sums(0, (0,), sums00)
         close_sums(0, (1,), sums01)
-        close_sums(0, (2, 3), sums02)
+        close_sums(0, (2,), sums02)
+        close_sums(0, (3,), sums03)
         st00 = room("st00", 1)
         st01 = room("st01", 1)
-        scopy(blocks(st01[:]), sums01)
+        st02 = room("st02", 1)
         weigh(0, blocks(st00[:]), sums00)
-        scatter_scalar(0, 0, 1, st00[:])
-        scatter_weighing(1, 0, 1, st01[:])
-        h1 = hidden(1, "bank2", (2, 3, 0, 1))
-        st02 = room("st02", 2, "wac1")
+        vcopy(blocks(st01[:]), sums01)
         weigh(0, blocks(st02[:]), sums02)
-        scatter_scalar(2, 0, 1, st02[:, own(0)])
-        scatter_scalar(3, 0, 1, st02[:, own(1)])
+        scatter_scalar(0, 0, 1, st00[:])
+        scatter_scalar(2, 0, 1, st02[:])
+        scatter_weighing(1, 0, 1, st01[:])
+        h1 = hidden(1, "bank1", (2, 3, 0, 1))
+        st03 = room("st03", 1, "wac1")
+        weigh(0, blocks(st03[:]), sums03)
+        scatter_scalar(3, 0, 1, st03[:])
 
         late = cast_pair(2, 1, vcopy)
         early = cast_pair(2, 0, vcopy)
         sums10 = open_sums(1, (0,), "bank0")
-        sums11 = open_sums(1, (1, 3), "bank1")
+        sums11 = open_sums(1, (1, 3), "bank2")
         sums12 = open_sums(1, (2,), "bank4")
         quantize_pair(2, 1, late)
         quantize_pair(2, 0, early)
@@ -321,14 +326,12 @@ def tile_moe_elr_gelu_kernel(tc, x_words, x_scales, w_words, w_scales, wa, wb_wo
         plain = sb([P, 2, E - 1, C], F32, "plain", "wac3")
         scopy(plain[:, 1:2, 0, :], sums11[:, 1:2, :])
         scatter_weighing(1, 1, 2, st11[:])
-        sums20 = products(2, (0,), "bank2")
-        sums30 = open_sums(3, (0,), "bank0")
+        sums20 = products(2, (0,), "bank1")
         sums21 = products(2, (1, 3), "bank3")
-        pair22 = psum.tile([P, PACK, C], F32, name="y_bank22", tag="bank5")
-        frozen(2, 2, pair22[:, 0, :])
-        adapter(2, 2, pair22[:, 0, :])
+        sums30 = open_sums(3, (0,), "bank0")
+        sums22 = products(2, (2,), "bank5")
         sums31 = open_sums(3, (1, 3), "bank7")
-        frozen(3, 2, pair22[:, 1, :])
+        sums32 = open_sums(3, (2,), "bank2")
         st20 = room("st20", 1)
         weigh(2, blocks(st20[:]), sums20)
         scatter_scalar(0, 2, 3, st20[:])
@@ -336,14 +339,15 @@ def tile_moe_elr_gelu_kernel(tc, x_words, x_scales, w_words, w_scales, wa, wb_wo
         quantize_hidden(3, h3, ws_plane[2][:, C : 2 * C])
         close_sums(3, (0,), sums30)
         close_sums(3, (1, 3), sums31)
-        adapter(3, 2, pair22[:, 1, :])
+        close_sums(3, (2,), sums32)
         vcopy(plain[:, :, 1, :], sums21)
         st30 = room("st30", 1)
         weigh(3, blocks(st30[:]), sums30)
+        weigh(2, weighted[:, 1:2, :], sums22)
         scatter_scalar(0, 3, 4, st30[:])
         store(0)
         vcopy(plain[:, :, 2, :], sums31)
-        nc.vector.tensor_tensor(weighted[:, 1:3, :], pair22[:, 0:2, :], blocks(gates[:, 2 * C : 4 * C]), MULT)
+        weigh(3, weighted[:, 2:3, :], sums32)
         scatter_weighing(1, 2, 4, plain[:, 0, 1:3, :].rearrange("p e c -> p (e c)"))
         store(1)
         scatter_scalar(2, 1, 4, weighted[:].rearrange("p e c -> p (e c)"))

@@ -24,8 +24,9 @@ QUADS = 4
 R = N // P
 LIST_COLS = C // 16
 ALIGN = 64
-SCALAR_M = 96
-HALF_M = P // 2
+SCALAR_M0 = 80
+SCALAR_M1 = 48
+QUARTER_M = P // 4
 
 
 def tile_moe_elr_gelu_kernel(tc, x_words, x_scales, w_words, w_scales, wa, wb_words, wb_scales, gate, offs, out):
@@ -50,7 +51,7 @@ def tile_moe_elr_gelu_kernel(tc, x_words, x_scales, w_words, w_scales, wa, wb_wo
         windows = [sb([P, T], F32, "window%d" % r) for r in range(R)]
         wa_raw = [sb([P, PACK, H], F32, "raw%d" % e) for e in range(E)]
         w_codes = {}
-        wb_codes = {}
+        wb_block = {}
 
         nc.vector.memset(xs_table[:].bitcast(I32), 0)
         nc.vector.memset(windows[0][:], 0.0)
@@ -76,7 +77,15 @@ def tile_moe_elr_gelu_kernel(tc, x_words, x_scales, w_words, w_scales, wa, wb_wo
             rows = wb_words[first:last, 0].rearrange("e p n d -> p e (n d)").bitcast(I32)
             nc.sync.dma_start(out=codes[:], in_=rows)
             for e in range(first, last):
-                wb_codes[e] = codes[:, e - first, :]
+                for r in range(R):
+                    wb_block[e, r] = codes[:, e - first, r * P : (r + 1) * P]
+
+        def load_wb_half(e, u):
+            codes = sb([P, N // 2], I32, "wb_half%d_%d" % (e, u))
+            rows = wb_words[e, 0, :, u * (N // 2) : (u + 1) * (N // 2), :].rearrange("p n d -> p (n d)").bitcast(I32)
+            nc.sync.dma_start(out=codes[:], in_=rows)
+            for r in (2 * u, 2 * u + 1):
+                wb_block[e, r] = codes[:, (r % 2) * P : (r % 2 + 1) * P]
 
         def load_xs(q):
             rows = x_scales[0, q:16:4, :].bitcast(I32)
@@ -110,9 +119,10 @@ def tile_moe_elr_gelu_kernel(tc, x_words, x_scales, w_words, w_scales, wa, wb_wo
         for q in range(QUADS):
             load_wbs(q)
         load_wa(2)
-        load_w(1, 2)
         load_wa(3)
-        load_wb(1, 2)
+        load_wb_half(1, 0)
+        load_w(1, 2)
+        load_wb_half(1, 1)
         load_wb(2, 3)
         load_ws(2, 4)
         load_w(2, 3)
@@ -125,8 +135,8 @@ def tile_moe_elr_gelu_kernel(tc, x_words, x_scales, w_words, w_scales, wa, wb_wo
         nc.vector.tensor_copy(word_scales[:], xs_table[:].indirect(offsets[:]))
 
         wa_codes = [sb([P, H], U32, "wac%d" % e) for e in range(E)]
-        wa_scales = [sb([P, H], U8, "was%d" % e) for e in range(E)]
-        wa_planes = {(e, u): wa_scales[e][:, 2 * u * P : 2 * (u + 1) * P] for e in range(E) for u in range(2)}
+        wa_scales = [sb([P, H], U8, "was%d" % e) for e in range(E - 1)]
+        wa_scales.append(w_codes[1][:, 0:H])
         h_codes = {}
         h_scales = {}
 
@@ -141,9 +151,9 @@ def tile_moe_elr_gelu_kernel(tc, x_words, x_scales, w_words, w_scales, wa, wb_wo
             copy(grouped[:, ts[0] : ts[1], ms[0] : ms[1], :].rearrange("p t m j -> p m j t"), source)
 
         def quantize(e, grouped, first, last):
-            codes = wa_codes[e][:, first * P : last * P].bitcast(FP8X4)
+            codes = wa_codes[e][:, first * P : last * P]
             values = grouped[:, first:last, :, :].rearrange("p t m j -> p (t m j)")
-            nc.vector.quantize_mx(out=codes, scales=wa_scales[e][:, first * P : last * P], in_=values)
+            nc.vector.quantize_mx(out=codes.bitcast(FP8X4), scales=wa_scales[e][:, first * P : last * P], in_=values)
 
         def cast_pair(e, u, copy, tag=None):
             pair = sb([P, 2, P, PACK], BF16, "pair%d_%d" % (e, u), tag)
@@ -151,12 +161,10 @@ def tile_moe_elr_gelu_kernel(tc, x_words, x_scales, w_words, w_scales, wa, wb_wo
             copy(pair[:].rearrange("p t m j -> p m j t"), source)
             return pair
 
-        def quantize_pair(e, u, pair, plane=None):
+        def quantize_pair(e, u, pair):
             cols = slice(2 * u * P, 2 * (u + 1) * P)
             values = pair[:].rearrange("p t m j -> p (t m j)")
-            if plane is not None:
-                wa_planes[e, u] = plane
-            nc.vector.quantize_mx(out=wa_codes[e][:, cols].bitcast(FP8X4), scales=wa_planes[e, u], in_=values)
+            nc.vector.quantize_mx(out=wa_codes[e][:, cols].bitcast(FP8X4), scales=wa_scales[e][:, cols], in_=values)
 
         def room(name, blocks, tag=None):
             return sb([P, blocks * C], F32, name, tag)
@@ -164,11 +172,10 @@ def tile_moe_elr_gelu_kernel(tc, x_words, x_scales, w_words, w_scales, wa, wb_wo
         def hidden(e, bank_tag, order, rounded=None):
             bank = psum.tile([P, PACK, C], F32, name="h_bank%d" % e, tag=bank_tag)
             for t in order:
-                cols = slice(t * P, (t + 1) * P)
                 nc.tensor.matmul_mx(
                     out=bank[:, t, :],
-                    lhsT=wa_codes[e][:, cols].bitcast(FP8X4),
-                    lhsT_scale=wa_planes[e, t // 2][:, (t % 2) * P : (t % 2 + 1) * P],
+                    lhsT=wa_codes[e][:, t * P : (t + 1) * P].bitcast(FP8X4),
+                    lhsT_scale=wa_scales[e][:, t * P : (t + 1) * P],
                     rhs=words[:, own(e)].bitcast(FP8X4),
                     rhs_scale=word_scales[:, own(e)],
                     start=True,
@@ -184,7 +191,7 @@ def tile_moe_elr_gelu_kernel(tc, x_words, x_scales, w_words, w_scales, wa, wb_wo
             h_scales[e] = sb([P, C], U8, "h_scales%d" % e)[:] if scales is None else scales
             nc.vector.quantize_mx(out=h_codes[e][:].bitcast(FP8X4), scales=h_scales[e], in_=rounded)
 
-        def frozen(e, r, sums, start=True):
+        def frozen(e, r, sums, start=True, stop=False):
             nc.tensor.matmul_mx(
                 out=sums,
                 lhsT=w_codes[e][:, 2 * r * P : 2 * (r + 1) * P].bitcast(FP4X4),
@@ -192,18 +199,18 @@ def tile_moe_elr_gelu_kernel(tc, x_words, x_scales, w_words, w_scales, wa, wb_wo
                 rhs=words[:, own(e)].bitcast(FP8X4),
                 rhs_scale=word_scales[:, own(e)],
                 start=start,
-                stop=False,
+                stop=stop,
             )
 
-        def adapter(e, r, sums, stop=True):
+        def adapter(e, r, sums, start=False, stop=True):
             cols = slice(r * P, (r + 1) * P)
             nc.tensor.matmul_mx(
                 out=sums,
-                lhsT=wb_codes[e][:, cols].bitcast(FP8X4),
+                lhsT=wb_block[e, r].bitcast(FP8X4),
                 lhsT_scale=wbs_plane[4 * e : P, cols],
                 rhs=h_codes[e][:].bitcast(FP8X4),
                 rhs_scale=h_scales[e],
-                start=False,
+                start=start,
                 stop=stop,
             )
 
@@ -217,12 +224,21 @@ def tile_moe_elr_gelu_kernel(tc, x_words, x_scales, w_words, w_scales, wa, wb_wo
             for i, r in enumerate(rows):
                 adapter(e, r, sums[:, i, :], stop=(i == len(rows) - 1))
 
-        def products(e, rows, bank_tag):
+        def products(e, rows, bank_tag, adapter_leads=False):
             bank = psum.tile([P, PACK, C], F32, name="y_bank%d_%d" % (e, rows[0]), tag=bank_tag)
             for i, r in enumerate(rows):
-                frozen(e, r, bank[:, i, :])
-                adapter(e, r, bank[:, i, :])
+                if adapter_leads:
+                    adapter(e, r, bank[:, i, :], start=True, stop=False)
+                    frozen(e, r, bank[:, i, :], start=False, stop=True)
+                else:
+                    frozen(e, r, bank[:, i, :])
+                    adapter(e, r, bank[:, i, :])
             return bank[:, 0 : len(rows), :]
+
+        def adapter_first(e, r, bank_tag):
+            bank = psum.tile([P, PACK, C], F32, name="y_bank%d_%d" % (e, r), tag=bank_tag)
+            adapter(e, r, bank[:, 0, :], start=True, stop=False)
+            return bank[:, 0:1, :]
 
         def blocks(flat):
             return flat.rearrange("p (b c) -> p b c", c=C)
@@ -236,9 +252,6 @@ def tile_moe_elr_gelu_kernel(tc, x_words, x_scales, w_words, w_scales, wa, wb_wo
 
         def scatter_weighing(r, first, last, values):
             nc.vector.tensor_tensor(windows[r][:].indirect(slots(first, last)), values, gates[:, first * C : last * C], MULT)
-
-        def scatter_vector(r, first, last, values):
-            nc.vector.tensor_copy(windows[r][:].indirect(slots(first, last)), values)
 
         def scatter_scalar(r, first, last, values):
             nc.scalar.activation(windows[r][:].indirect(slots(first, last)), values, COPY)
@@ -257,8 +270,8 @@ def tile_moe_elr_gelu_kernel(tc, x_words, x_scales, w_words, w_scales, wa, wb_wo
 
         grouped = rounded_tile(0)
         cast(0, grouped, (2, 4), (0, P), vcopy)
-        cast(0, grouped, (0, 2), (0, SCALAR_M), scopy)
-        cast(0, grouped, (0, 2), (SCALAR_M, P), vcopy)
+        cast(0, grouped, (0, 2), (0, SCALAR_M0), scopy)
+        cast(0, grouped, (0, 2), (SCALAR_M0, P), vcopy)
         quantize(0, grouped, 2, 4)
         quantize(0, grouped, 0, 1)
         quantize(0, grouped, 1, 2)
@@ -266,14 +279,14 @@ def tile_moe_elr_gelu_kernel(tc, x_words, x_scales, w_words, w_scales, wa, wb_wo
         h0 = hidden(0, "bank0", (2, 3, 0, 1))
 
         grouped = rounded_tile(1)
-        cast(1, grouped, (0, 4), (SCALAR_M, P), vcopy)
-        cast(1, grouped, (2, 4), (0, SCALAR_M), vcopy)
+        cast(1, grouped, (2, 4), (0, P), vcopy)
+        cast(1, grouped, (0, 2), (SCALAR_M1, P), vcopy)
         sums00 = open_sums(0, (0,), "bank1")
         sums01 = open_sums(0, (1,), "bank2")
         sums02 = open_sums(0, (2,), "bank3")
         sums03 = open_sums(0, (3,), "bank4")
         quantize_hidden(0, h0, ws_plane[0][:, 0:C])
-        cast(1, grouped, (0, 2), (0, SCALAR_M), scopy)
+        cast(1, grouped, (0, 2), (0, SCALAR_M1), scopy)
         quantize(1, grouped, 2, 4)
         quantize(1, grouped, 0, 1)
         quantize(1, grouped, 1, 2)
@@ -297,53 +310,56 @@ def tile_moe_elr_gelu_kernel(tc, x_words, x_scales, w_words, w_scales, wa, wb_wo
 
         late = cast_pair(2, 1, vcopy)
         early = cast_pair(2, 0, vcopy)
-        sums10 = open_sums(1, (0,), "bank0")
-        sums11 = open_sums(1, (1, 3), "bank2")
-        sums12 = open_sums(1, (2,), "bank4")
         quantize_pair(2, 1, late)
         quantize_pair(2, 0, early)
         quantize_hidden(1, h1, tag="pair2_1")
 
         grouped = rounded_tile(3)
-        cast(3, grouped, (0, 4), (0, HALF_M), vcopy)
-        cast(3, grouped, (0, 2), (HALF_M, P), scopy)
-        cast(3, grouped, (2, 4), (HALF_M, P), vcopy)
-        h2 = hidden(2, "bank5", (2, 3, 0, 1), wa_raw[3][:, 0, 0 : H // 2].bitcast(BF16))
-        close_sums(1, (0,), sums10)
-        close_sums(1, (1, 3), sums11)
-        close_sums(1, (2,), sums12)
-        quantize(3, grouped, 0, 2)
+        cast(3, grouped, (0, 4), (0, QUARTER_M), vcopy)
+        cast(3, grouped, (0, 4), (P - QUARTER_M, P), scopy)
+        cast(3, grouped, (0, 4), (QUARTER_M, P - QUARTER_M), vcopy)
+        spent = wa_raw[3][:].rearrange("p j c -> p (j c)")[:, H - C : H + C]
+        h2 = hidden(2, "bank5", (2, 3, 0, 1), spent.bitcast(BF16))
+        sums10 = adapter_first(1, 0, "bank0")
+        sums11 = adapter_first(1, 1, "bank2")
+        frozen(1, 0, sums10[:, 0, :], start=False, stop=True)
+        frozen(1, 1, sums11[:, 0, :], start=False, stop=True)
+        sums12 = adapter_first(1, 2, "bank4")
+        frozen(1, 2, sums12[:, 0, :], start=False, stop=True)
+        sums13 = adapter_first(1, 3, "bank3")
+        frozen(1, 3, sums13[:, 0, :], start=False, stop=True)
         st10 = room("st10", 1)
         weigh(1, blocks(st10[:]), sums10)
-        st11 = room("st11", 1)
-        weighted = sb([P, E - 1, C], F32, "weighted")
-        scopy(blocks(st11[:]), sums11[:, 0:1, :])
         scatter_scalar(0, 1, 2, st10[:])
+        quantize(3, grouped, 0, 2)
         quantize(3, grouped, 2, 3)
         quantize(3, grouped, 3, 4)
+        st11 = room("st11", 1)
+        vcopy(blocks(st11[:]), sums11)
+        quantize_hidden(2, h2, tag="grouped3")
         h3 = hidden(3, "bank6", (0, 1, 2, 3))
-        quantize_hidden(2, h2)
         plain = sb([P, 2, E - 1, C], F32, "plain", "wac3")
-        scopy(plain[:, 1:2, 0, :], sums11[:, 1:2, :])
+        scopy(plain[:, 1:2, 0, :], sums13)
         scatter_weighing(1, 1, 2, st11[:])
-        sums20 = products(2, (0,), "bank1")
-        sums21 = products(2, (1, 3), "bank3")
-        sums30 = open_sums(3, (0,), "bank0")
-        sums22 = products(2, (2,), "bank5")
-        sums31 = open_sums(3, (1, 3), "bank7")
-        sums32 = open_sums(3, (2,), "bank2")
+        sums20 = open_sums(2, (0,), "bank1")
+        sums21 = open_sums(2, (1, 3), "bank5")
+        close_sums(2, (0,), sums20)
+        close_sums(2, (1, 3), sums21)
         st20 = room("st20", 1)
         weigh(2, blocks(st20[:]), sums20)
         scatter_scalar(0, 2, 3, st20[:])
-        weigh(1, weighted[:, 0:1, :], sums12)
-        quantize_hidden(3, h3, ws_plane[2][:, C : 2 * C])
+        sums30 = open_sums(3, (0,), "bank0")
+        sums22 = products(2, (2,), "bank6")
+        quantize_hidden(3, h3, wb_block[2, 1].bitcast(U8)[:, 0:C])
         close_sums(3, (0,), sums30)
-        close_sums(3, (1, 3), sums31)
-        close_sums(3, (2,), sums32)
+        sums31 = products(3, (1, 3), "bank7", adapter_leads=True)
+        sums32 = products(3, (2,), "bank2", adapter_leads=True)
+        weighted = sb([P, E - 1, C], F32, "weighted", "h3")
+        weigh(1, weighted[:, 0:1, :], sums12)
         vcopy(plain[:, :, 1, :], sums21)
+        weigh(2, weighted[:, 1:2, :], sums22)
         st30 = room("st30", 1)
         weigh(3, blocks(st30[:]), sums30)
-        weigh(2, weighted[:, 1:2, :], sums22)
         scatter_scalar(0, 3, 4, st30[:])
         store(0)
         vcopy(plain[:, :, 2, :], sums31)

from contextlib import ExitStack

import concourse.mybir as mybir
from concourse.masks import make_identity

K, T, E, C, H, N = 512, 1024, 4, 128, 512, 512
FLOPS = 2 * E * C * (K * H + K * N + H * N)

F32 = mybir.dt.float32
BF16 = mybir.dt.bfloat16
I32 = mybir.dt.int32
U32 = mybir.dt.uint32
U16 = mybir.dt.uint16
U8 = mybir.dt.uint8
FP8X4 = mybir.dt.float8_e4m3fn_x4
FP4X4 = mybir.dt.float4_e2m1fn_x4
GELU = mybir.ActivationFunctionType.Gelu_apprx_tanh
COPY = mybir.ActivationFunctionType.Copy
MULT = mybir.AluOpType.mult

P = 128
PACK = 4
QUADS = 4
R = N // P
LIST_COLS = C // 16
ALIGN = 64
SCALAR_M0 = 80
SCALAR_M1 = 48
QUARTER_M = P // 4


def tile_moe_elr_gelu_kernel(tc, x_words, x_scales, w_words, w_scales, wa, wb_words, wb_scales, gate, offs, out):
    nc = tc.nc
    with ExitStack() as ctx:
        keep = ctx.enter_context(tc.tile_pool(name="keep", bufs=1))
        psum = ctx.enter_context(tc.psum_pool(name="psum", bufs=1))

        def sb(shape, dtype, name, tag=None):
            return keep.tile(shape, dtype, name=name, tag=tag or name, align_bytes=ALIGN)

        offsets = keep.tile([P, E * LIST_COLS], U16, name="offsets")
        x_table = sb([P, T], I32, "x_table")
        xs_table = sb([P, T], U8, "xs_table")
        ws_halves = [sb([P, 2, N], U8, "ws_plane%d" % i) for i in range(2)]
        ws_plane = [ws_halves[e // 2][:, e % 2, :] for e in range(E)]
        wbs_plane = sb([P, N], U8, "wbs_plane")
        gate_cols = sb([P, PACK], F32, "gate_cols")
        gates = sb([P, E * C], F32, "gates")
        identity = sb([P, P], F32, "identity")
        make_identity(nc, identity[:])
        windows = [sb([P, T], F32, "window%d" % r) for r in range(R)]
        wa_raw = [sb([P, PACK, H], F32, "raw%d" % e) for e in range(E)]
        w_codes = {}
        wb_block = {}

        nc.vector.memset(xs_table[:].bitcast(I32), 0)
        nc.vector.memset(windows[0][:], 0.0)
        nc.vector.memset(ws_halves[0][:].rearrange("p e n -> p (e n)").bitcast(I32), 0)
        nc.vector.memset(wbs_plane[:].bitcast(I32), 0)
        nc.vector.memset(ws_halves[1][:].rearrange("p e n -> p (e n)").bitcast(I32), 0)
        nc.vector.tensor_copy(windows[1][:], windows[0][:])
        for r in (2, 3):
            nc.scalar.activation(windows[r][:], windows[0][:], GELU)

        def load_wa(e):
            nc.sync.dma_start(out=wa_raw[e][:], in_=wa[e].rearrange("(p j) c -> p j c", j=PACK))

        def load_w(first, last):
            codes = sb([P, last - first, 2 * N], U8, "w_codes%d" % first)
            rows = w_words[first:last, 0].bitcast(I32).rearrange("e p n -> p e n")
            nc.sync.dma_start(out=codes[:].bitcast(I32), in_=rows)
            for e in range(first, last):
                w_codes[e] = codes[:, e - first, :]

        def load_wb(first, last):
            codes = sb([P, last - first, N], I32, "wb_codes%d" % first)
            rows = wb_words[first:last, 0].rearrange("e p n d -> p e (n d)").bitcast(I32)
            nc.sync.dma_start(out=codes[:], in_=rows)
            for e in range(first, last):
                for r in range(R):
                    wb_block[e, r] = codes[:, e - first, r * P : (r + 1) * P]

        def load_wb_half(e, u):
            codes = sb([P, N // 2], I32, "wb_half%d_%d" % (e, u))
            rows = wb_words[e, 0, :, u * (N // 2) : (u + 1) * (N // 2), :].rearrange("p n d -> p (n d)").bitcast(I32)
            nc.sync.dma_start(out=codes[:], in_=rows)
            for r in (2 * u, 2 * u + 1):
                wb_block[e, r] = codes[:, (r % 2) * P : (r % 2 + 1) * P]

        def load_xs(q):
            rows = x_scales[0, q:16:4, :].bitcast(I32)
            nc.sync.dma_start(out=xs_table[q:P:32, :].bitcast(I32), in_=rows)

        def load_ws(first, last):
            for q in range(QUADS):
                rows = w_scales[first:last, 0, q:16:4, :].bitcast(I32).rearrange("e b n -> b e n")
                nc.sync.dma_start(out=ws_halves[first // 2][q:P:32, first % 2 : first % 2 + last - first, :].bitcast(I32), in_=rows)

        def load_wbs(q):
            rows = wb_scales[:, 0, 4 * q : 4 * q + 4, :].bitcast(I32)
            nc.sync.dma_start(out=wbs_plane[32 * q : 32 * q + 16, :].bitcast(I32), in_=rows)

        def load_x():
            nc.sync.dma_start(out=x_table[:], in_=x_words[0].rearrange("p t d -> p (t d)").bitcast(I32))

        def load_gate():
            nc.sync.dma_start(out=gate_cols[:], in_=gate[0].rearrange("(p t) -> p t", t=PACK))

        load_x()
        nc.sync.dma_start(offsets[:], offs)
        for q in range(QUADS):
            load_xs(q)
        load_wa(0)
        load_gate()
        load_ws(0, 2)
        load_wa(1)
        load_w(0, 1)
        load_wb(0, 1)
        for q in range(QUADS):
            load_wbs(q)
        load_wa(2)
        load_wa(3)
        load_wb_half(1, 0)
        load_w(1, 2)
        load_wb_half(1, 1)
        load_wb(2, 3)
        load_ws(2, 4)
        load_w(2, 3)
        load_w(3, 4)
        load_wb(3, 4)

        words = sb([P, E * C], U32, "slot_words")
        word_scales = sb([P, E * C], U8, "slot_scales")
        nc.vector.tensor_copy(words[:], x_table[:].bitcast(U32).indirect(offsets[:]))
        nc.vector.tensor_copy(word_scales[:], xs_table[:].indirect(offsets[:]))

        wa_codes = [sb([P, H], U32, "wac%d" % e) for e in range(E)]
        wa_scales = [sb([P, H], U8, "was%d" % e) for e in range(E - 1)]
        wa_scales.append(w_codes[1][:, 0:H])
        h_codes = {}
        h_scales = {}

        def own(e):
            return slice(e * C, (e + 1) * C)

        def rounded_tile(e, tag=None):
            return sb([P, PACK, P, PACK], BF16, "grouped%d" % e, tag)

        def cast(e, grouped, ts, ms, copy):
            source = wa_raw[e][:].rearrange("p j (m t) -> p m j t", t=PACK)[:, ms[0] : ms[1], :, ts[0] : ts[1]]
            copy(grouped[:, ts[0] : ts[1], ms[0] : ms[1], :].rearrange("p t m j -> p m j t"), source)

        def quantize(e, grouped, first, last):
            codes = wa_codes[e][:, first * P : last * P]
            values = grouped[:, first:last, :, :].rearrange("p t m j -> p (t m j)")
            nc.vector.quantize_mx(out=codes.bitcast(FP8X4), scales=wa_scales[e][:, first * P : last * P], in_=values)

        def cast_pair(e, u, copy, tag=None):
            pair = sb([P, 2, P, PACK], BF16, "pair%d_%d" % (e, u), tag)
            source = wa_raw[e][:].rearrange("p j (m t) -> p m j t", t=PACK)[:, :, :, 2 * u : 2 * u + 2]
            copy(pair[:].rearrange("p t m j -> p m j t"), source)
            return pair

        def quantize_pair(e, u, pair):
            cols = slice(2 * u * P, 2 * (u + 1) * P)
            values = pair[:].rearrange("p t m j -> p (t m j)")
            nc.vector.quantize_mx(out=wa_codes[e][:, cols].bitcast(FP8X4), scales=wa_scales[e][:, cols], in_=values)

        def room(name, blocks, tag=None):
            return sb([P, blocks * C], F32, name, tag)

        def hidden(e, bank_tag, order, rounded=None):
            bank = psum.tile([P, PACK, C], F32, name="h_bank%d" % e, tag=bank_tag)
            for t in order:
                nc.tensor.matmul_mx(
                    out=bank[:, t, :],
                    lhsT=wa_codes[e][:, t * P : (t + 1) * P].bitcast(FP8X4),
                    lhsT_scale=wa_scales[e][:, t * P : (t + 1) * P],
                    rhs=words[:, own(e)].bitcast(FP8X4),
                    rhs_scale=word_scales[:, own(e)],
                    start=True,
                    stop=True,
                )
            if rounded is None:
                rounded = room("h%d" % e, 2)[:].bitcast(BF16)
            nc.scalar.activation(rounded.rearrange("p (n t) -> p n t", t=PACK), bank[:].rearrange("p t n -> p n t"), GELU)
            return rounded

        def quantize_hidden(e, rounded, scales=None, tag=None):
            h_codes[e] = sb([P, C], U32, "h_codes%d" % e, tag)
            h_scales[e] = sb([P, C], U8, "h_scales%d" % e)[:] if scales is None else scales
            nc.vector.quantize_mx(out=h_codes[e][:].bitcast(FP8X4), scales=h_scales[e], in_=rounded)

        def frozen(e, r, sums, start=True, stop=False):
            nc.tensor.matmul_mx(
                out=sums,
                lhsT=w_codes[e][:, 2 * r * P : 2 * (r + 1) * P].bitcast(FP4X4),
                lhsT_scale=ws_plane[e][:, r * P : (r + 1) * P],
                rhs=words[:, own(e)].bitcast(FP8X4),
                rhs_scale=word_scales[:, own(e)],
                start=start,
                stop=stop,
            )

        def adapter(e, r, sums, start=False, stop=True):
            cols = slice(r * P, (r + 1) * P)
            nc.tensor.matmul_mx(
                out=sums,
                lhsT=wb_block[e, r].bitcast(FP8X4),
                lhsT_scale=wbs_plane[4 * e : P, cols],
                rhs=h_codes[e][:].bitcast(FP8X4),
                rhs_scale=h_scales[e],
                start=start,
                stop=stop,
            )

        def open_sums(e, rows, bank_tag):
            bank = psum.tile([P, PACK, C], F32, name="y_bank%d_%d" % (e, rows[0]), tag=bank_tag)
            for i, r in enumerate(rows):
                frozen(e, r, bank[:, i, :], start=(i == 0))
            return bank[:, 0 : len(rows), :]

        def close_sums(e, rows, sums):
            for i, r in enumerate(rows):
                adapter(e, r, sums[:, i, :], stop=(i == len(rows) - 1))

        def products(e, rows, bank_tag, adapter_leads=False):
            bank = psum.tile([P, PACK, C], F32, name="y_bank%d_%d" % (e, rows[0]), tag=bank_tag)
            for i, r in enumerate(rows):
                if adapter_leads:
                    adapter(e, r, bank[:, i, :], start=True, stop=False)
                    frozen(e, r, bank[:, i, :], start=False, stop=True)
                else:
                    frozen(e, r, bank[:, i, :])
                    adapter(e, r, bank[:, i, :])
            return bank[:, 0 : len(rows), :]

        def adapter_first(e, r, bank_tag):
            bank = psum.tile([P, PACK, C], F32, name="y_bank%d_%d" % (e, r), tag=bank_tag)
            adapter(e, r, bank[:, 0, :], start=True, stop=False)
            return bank[:, 0:1, :]

        def blocks(flat):
            return flat.rearrange("p (b c) -> p b c", c=C)

        def weigh(e, target, sums):
            weights = gates[:, own(e)].unsqueeze(1).to_broadcast(list(sums.shape))
            nc.vector.tensor_tensor(target, sums, weights, MULT)

        def slots(first, last):
            return offsets[:, first * LIST_COLS : last * LIST_COLS]

        def scatter_weighing(r, first, last, values):
            nc.vector.tensor_tensor(windows[r][:].indirect(slots(first, last)), values, gates[:, first * C : last * C], MULT)

        def scatter_scalar(r, first, last, values):
            nc.scalar.activation(windows[r][:].indirect(slots(first, last)), values, COPY)

        def store(r):
            nc.sync.dma_start(out=out[r * P : (r + 1) * P, :], in_=windows[r][:])

        def spread_gates(bank_tag):
            spread = psum.tile([P, PACK, P], F32, name="gate_bank", tag=bank_tag)
            for t in range(PACK):
                nc.tensor.transpose(spread[:, t, :], gate_cols[:, t : t + 1].to_broadcast([P, P]), identity[:])
            nc.scalar.copy(gates[:].rearrange("p (n t) -> p n t", t=PACK), spread[:].rearrange("p t n -> p n t"))

        vcopy = nc.vector.tensor_copy
        scopy = nc.scalar.copy

        grouped = rounded_tile(0)
        cast(0, grouped, (2, 4), (0, P), vcopy)
        cast(0, grouped, (0, 2), (0, SCALAR_M0), scopy)
        cast(0, grouped, (0, 2), (SCALAR_M0, P), vcopy)
        quantize(0, grouped, 2, 4)
        quantize(0, grouped, 0, 1)
        quantize(0, grouped, 1, 2)
        spread_gates("bank7")
        h0 = hidden(0, "bank0", (2, 3, 0, 1))

        grouped = rounded_tile(1)
        cast(1, grouped, (2, 4), (0, P), vcopy)
        cast(1, grouped, (0, 2), (SCALAR_M1, P), vcopy)
        sums00 = open_sums(0, (0,), "bank1")
        sums01 = open_sums(0, (1,), "bank2")
        sums02 = open_sums(0, (2,), "bank3")
        sums03 = open_sums(0, (3,), "bank4")
        quantize_hidden(0, h0, ws_plane[0][:, 0:C])
        cast(1, grouped, (0, 2), (0, SCALAR_M1), scopy)
        quantize(1, grouped, 2, 4)
        quantize(1, grouped, 0, 1)
        quantize(1, grouped, 1, 2)
        close_sums(0, (0,), sums00)
        close_sums(0, (1,), sums01)
        close_sums(0, (2,), sums02)
        close_sums(0, (3,), sums03)
        st00 = room("st00", 1)
        st01 = room("st01", 1)
        st02 = room("st02", 1)
        weigh(0, blocks(st00[:]), sums00)
        vcopy(blocks(st01[:]), sums01)
        weigh(0, blocks(st02[:]), sums02)
        scatter_scalar(0, 0, 1, st00[:])
        scatter_scalar(2, 0, 1, st02[:])
        scatter_weighing(1, 0, 1, st01[:])
        h1 = hidden(1, "bank1", (2, 3, 0, 1))
        st03 = room("st03", 1, "wac1")
        weigh(0, blocks(st03[:]), sums03)
        scatter_scalar(3, 0, 1, st03[:])

        late = cast_pair(2, 1, vcopy)
        early = cast_pair(2, 0, vcopy)
        quantize_pair(2, 1, late)
        quantize_pair(2, 0, early)
        quantize_hidden(1, h1, tag="pair2_1")

        grouped = rounded_tile(3)
        cast(3, grouped, (0, 4), (0, QUARTER_M), vcopy)
        cast(3, grouped, (0, 4), (P - QUARTER_M, P), scopy)
        cast(3, grouped, (0, 4), (QUARTER_M, P - QUARTER_M), vcopy)
        spent = wa_raw[3][:].rearrange("p j c -> p (j c)")[:, H - C : H + C]
        h2 = hidden(2, "bank5", (2, 3, 0, 1), spent.bitcast(BF16))
        sums10 = adapter_first(1, 0, "bank0")
        sums11 = adapter_first(1, 1, "bank2")
        frozen(1, 0, sums10[:, 0, :], start=False, stop=True)
        frozen(1, 1, sums11[:, 0, :], start=False, stop=True)
        sums12 = adapter_first(1, 2, "bank4")
        frozen(1, 2, sums12[:, 0, :], start=False, stop=True)
        sums13 = adapter_first(1, 3, "bank3")
        frozen(1, 3, sums13[:, 0, :], start=False, stop=True)
        st10 = room("st10", 1)
        weigh(1, blocks(st10[:]), sums10)
        scatter_scalar(0, 1, 2, st10[:])
        quantize(3, grouped, 0, 2)
        quantize(3, grouped, 2, 3)
        quantize(3, grouped, 3, 4)
        st11 = room("st11", 1)
        vcopy(blocks(st11[:]), sums11)
        quantize_hidden(2, h2, tag="grouped3")
        h3 = hidden(3, "bank6", (0, 1, 2, 3))
        plain = sb([P, 2, E - 1, C], F32, "plain", "wac3")
        scopy(plain[:, 1:2, 0, :], sums13)
        scatter_weighing(1, 1, 2, st11[:])
        sums20 = open_sums(2, (0,), "bank1")
        sums21 = open_sums(2, (1, 3), "bank5")
        close_sums(2, (0,), sums20)
        close_sums(2, (1, 3), sums21)
        st20 = room("st20", 1)
        weigh(2, blocks(st20[:]), sums20)
        scatter_scalar(0, 2, 3, st20[:])
        sums30 = open_sums(3, (0,), "bank0")
        sums22 = products(2, (2,), "bank6")
        quantize_hidden(3, h3, wb_block[2, 1].bitcast(U8)[:, 0:C])
        close_sums(3, (0,), sums30)
        sums31 = products(3, (1, 3), "bank7", adapter_leads=True)
        sums32 = products(3, (2,), "bank2", adapter_leads=True)
        weighted = sb([P, E - 1, C], F32, "weighted", "h3")
        weigh(1, weighted[:, 0:1, :], sums12)
        vcopy(plain[:, :, 1, :], sums21)
        weigh(2, weighted[:, 1:2, :], sums22)
        st30 = room("st30", 1)
        weigh(3, blocks(st30[:]), sums30)
        scatter_scalar(0, 3, 4, st30[:])
        store(0)
        vcopy(plain[:, :, 2, :], sums31)
        weigh(3, weighted[:, 2:3, :], sums32)
        scatter_weighing(1, 2, 4, plain[:, 0, 1:3, :].rearrange("p e c -> p (e c)"))
        store(1)
        scatter_scalar(2, 1, 4, weighted[:].rearrange("p e c -> p (e c)"))
        store(2)
        scatter_weighing(3, 1, 4, plain[:, 1, :, :].rearrange("p e c -> p (e c)"))
        store(3)
